import numpy as np
import ml_dtypes


def mxq(x, axis, fmt="e4m3"):
    dtype, down = {"e4m3": (ml_dtypes.float8_e4m3fn, 7), "e5m2": (ml_dtypes.float8_e5m2, 14)}[fmt]
    v = np.moveaxis(np.asarray(x, np.float32).astype(ml_dtypes.bfloat16).astype(np.float64), axis, -1)
    blocks = v.reshape(v.shape[:-1] + (-1, 32))
    amax = np.abs(blocks).max(-1, keepdims=True)
    byte = np.maximum(np.where(amax > 0, np.frexp(amax)[1] - 1 + 127, 0) - down, 1)
    scale = np.exp2(byte - 127.0)
    codes = (blocks / scale).astype(np.float32).astype(dtype).astype(np.float64)
    return np.moveaxis((codes * scale).reshape(v.shape), -1, axis)


WIDE = False


def mx_kscale(k):
    if not WIDE:
        return np.ones(k)
    levels = np.array([10, -10, 5, -5, 0])
    if k % 512:
        return np.exp2(np.random.permutation(np.resize(levels, k // 32))).repeat(32)
    a = np.empty((k // 512, 16))
    for p in range(k // 512):
        a[p, :8] = np.random.permutation(np.resize(levels, 8))
        for g in range(8):
            far = levels[np.abs(levels - a[p, g]) >= 10]
            a[p, g + 8] = far[np.random.randint(len(far))]
    return np.exp2(a.ravel()).repeat(32)


def f64(x):
    return np.asarray(x).astype(np.float64)


def striped8(idx):
    return np.concatenate([v.reshape(-1, 16).T for v in idx]).astype(np.uint16)


def unstriped8(offs):
    return np.stack([offs[16 * g:16 * g + 16].T.reshape(-1) for g in range(8)]).astype(np.int64)


E2M1 = np.array([0.0, 0.5, 1.0, 1.5, 2.0, 3.0, 4.0, 6.0, -0.0, -0.5, -1.0, -1.5, -2.0, -3.0, -4.0, -6.0])


def pack_weight(w, fmt):
    k, n = w.shape
    w = f64(np.asarray(w, np.float32).astype(ml_dtypes.bfloat16)).reshape(k // 32, 32, n)
    amax = np.abs(w).max(1)
    if fmt == "e4m3":
        byte = np.frexp(amax)[1] - 1 + 127 - 7
    else:
        mant, ex = np.frexp(amax / 6.0)
        byte = np.where(mant > 0.5, ex, ex - 1) + 127
    byte = np.clip(np.where(amax > 0, byte, 1), 1, 254)
    scaled = (w * np.exp2(127.0 - byte)[:, None, :]).reshape(k, n).astype(np.float32)
    by_word = np.ascontiguousarray(scaled.reshape(k // 512, 128, 4, n).transpose(0, 1, 3, 2))
    if fmt == "e4m3":
        words = by_word.astype(ml_dtypes.float8_e4m3fn).view(np.uint8)
    else:
        c = by_word.astype(ml_dtypes.float4_e2m1fn).view(np.uint8) & 0xF
        words = (c[..., 0::2] | (c[..., 1::2] << 4)).reshape(k // 512, 128, 2 * n)
    return np.ascontiguousarray(words), np.ascontiguousarray(byte.astype(np.uint8).reshape(k // 512, 16, n))


def unpack_weight(words, scales, fmt):
    g, _, n = scales.shape
    words = np.ascontiguousarray(words).reshape(g, 128, n, -1)
    if fmt == "e4m3":
        vals = words.view(ml_dtypes.float8_e4m3fn).astype(np.float64)
    else:
        nib = np.empty((g, 128, n, 4), np.uint8)
        nib[..., 0::2] = words & 0xF
        nib[..., 1::2] = words >> 4
        vals = E2M1[nib]
    vals = vals * np.repeat(np.exp2(scales.astype(np.float64) - 127.0), 8, axis=1)[..., None]
    return vals.transpose(0, 1, 3, 2).reshape(g * 512, n)


K, M, T, S = 1024, 1024, 1024, 512


def setup_inputs():
    n = np.random.standard_normal
    s = mx_kscale(K)[:, None]
    p_w = pack_weight(n((K, M)) / np.sqrt(K) / s, "e2m1")
    return {
        "xT": (n((K, T)) * s).astype(np.float32),
        "w_words": p_w[0],
        "w_scales": p_w[1],
        "wgt": np.repeat(np.random.uniform(0.5, 2.0, (8, S)), 16, axis=0).astype(np.float32),
        "wgo": np.repeat(np.random.uniform(0.5, 2.0, (8, S)), 16, axis=0).astype(np.float32),
        "offs": striped8(np.stack([np.random.permutation(T)[:S] for _ in range(8)])),
        "offs2": striped8(np.stack([np.random.permutation(T)[:S] for _ in range(8)])),
    }


def reference(xT, w_words, w_scales, wgt, wgo, offs, offs2):
    idx = unstriped8(offs)
    group = np.arange(K) % 512 // 64
    xg = f64(wgt)[np.arange(K) // 4 % 128] * f64(xT)[np.arange(K)[:, None], idx[group]]
    xT_ = mxq(xg, 0, "e4m3")
    w_ = unpack_weight(w_words, w_scales, "e2m1")
    y = w_.T @ xT_
    place = unstriped8(offs2)[np.arange(M) % 128 // 16]
    out = np.zeros((M, T))
    out[np.arange(M)[:, None], place] = f64(wgo)[np.arange(M) % 128] * (y)
    return out

@@ -1,0 +1,147 @@
+import concourse.mybir as mybir
+
+K, M, T, S = 1024, 1024, 1024, 512
+FLOPS = 2 * K * M * S
+
+F32 = mybir.dt.float32
+BF16 = mybir.dt.bfloat16
+I32 = mybir.dt.int32
+U32 = mybir.dt.uint32
+U16 = mybir.dt.uint16
+U8 = mybir.dt.uint8
+FP8X4 = mybir.dt.float8_e4m3fn_x4
+FP4X4 = mybir.dt.float4_e2m1fn_x4
+MULT = mybir.AluOpType.mult
+
+P = 128
+PACK = 4
+PASSES = K // (P * PACK)
+BLOCKS = M // P
+HALF = S // 2
+CHUNK = 128
+OFF_COLS = HALF // 16
+
+
+def tile_list_hboth_none_kernel(tc, xT, w_words, w_scales, wgt, wgo, offs, offs2, out):
+    nc = tc.nc
+    with tc.tile_pool(name="held", bufs=1) as held, tc.psum_pool(name="psum", bufs=1) as psum:
+        list_in = held.tile([P, S // 16], U16, name="list_in")
+        list_out = held.tile([P, S // 16], U16, name="list_out")
+        wgt_sb = held.tile([P, S], F32, name="wgt_sb")
+        wgo_sb = held.tile([P, S], F32, name="wgo_sb")
+        w_sb = held.tile([P, PASSES, 2 * M], U8, name="w_sb", align_bytes=64)
+        wsc = held.tile([P, PASSES, M], U8, name="wsc", align_bytes=64)
+        plane = [[held.tile([P, T], F32, name=f"plane{a}_{t}") for t in range(PACK)] for a in range(PASSES)]
+        picked = [[held.tile([P, PACK, HALF], F32, name=f"picked{a}_{h}") for h in range(2)] for a in range(PASSES)]
+        grouped = [[held.tile([P, HALF, PACK], BF16, name=f"grouped{a}_{h}", align_bytes=64) for h in range(2)] for a in range(PASSES)]
+        codes = [[held.tile([P, HALF], U32, name=f"codes{a}_{h}", align_bytes=64) for h in range(2)] for a in range(PASSES)]
+        xsc = [[held.tile([P, HALF], U8, name=f"xsc{a}_{h}", align_bytes=64) for h in range(2)] for a in range(PASSES)]
+        window = [held.tile([P, T], F32, name=f"window{b}") for b in range(BLOCKS)]
+        y_sb = [held.tile([P, S], F32, name=f"y{b}") for b in range(BLOCKS)]
+        bank = [psum.tile([P, S], F32, name=f"bank{b}") for b in range(BLOCKS)]
+
+        nc.gpsimd.memset(wsc[:].bitcast(I32), 0)
+        for b in range(BLOCKS):
+            nc.vector.memset(window[b][:] if b < 4 else window[b][:, 0:8], 0.0)
+        for b in range(4, BLOCKS):
+            nc.gpsimd.memset(window[b][:], 0.0)
+
+        rows = xT.rearrange("(a p t) n -> a t p n", p=P, t=PACK)
+        nc.sync.dma_start(list_in[:], offs)
+        nc.sync.dma_start(plane[0][0][:], rows[0, 0])
+        nc.scalar.dma_start(wgt_sb[:, 0:HALF], wgt[:, 0:HALF])
+        nc.sync.dma_start(wgt_sb[:, HALF:S], wgt[:, HALF:S])
+        for a in range(PASSES):
+            for t in range(PACK):
+                if a + t > 0:
+                    nc.sync.dma_start(plane[a][t][:], rows[a, t])
+        nc.sync.dma_start(w_sb[:].bitcast(I32), w_words.bitcast(I32).rearrange("a p n -> p a n"))
+        for q in range(4):
+            nc.sync.dma_start(
+                wsc[32 * q : 32 * q + 4].bitcast(I32),
+                w_scales.bitcast(I32)[:, 4 * q : 4 * q + 4, :].rearrange("a r n -> r a n"),
+            )
+        nc.sync.dma_start(list_out[:], offs2)
+        nc.sync.dma_start(wgo_sb[:], wgo)
+
+        def gather(a, t, h):
+            nc.vector.tensor_tensor(
+                picked[a][h][:, t, :],
+                plane[a][t][:].indirect(list_in[:, h * OFF_COLS : (h + 1) * OFF_COLS]),
+                wgt_sb[:, h * HALF : (h + 1) * HALF],
+                MULT,
+            )
+
+        def views(a, h, lo, hi):
+            return grouped[a][h][:, lo:hi, :], picked[a][h][:, :, lo:hi].rearrange("p t c -> p c t")
+
+        def interleave_scalar(a, h, lo, hi):
+            dst, src = views(a, h, lo, hi)
+            nc.scalar.copy(dst, src)
+
+        def interleave_vector(a, h, lo, hi):
+            dst, src = views(a, h, lo, hi)
+            nc.vector.tensor_copy(dst, src)
+
+        def quantize(a, h, lo, hi):
+            nc.vector.quantize_mx(
+                out=codes[a][h][:, lo:hi].bitcast(FP8X4),
+                scales=xsc[a][h][:, lo:hi],
+                in_=grouped[a][h][:, lo:hi, :].rearrange("p c t -> p (c t)"),
+            )
+
+        def multiply(b, h):
+            for c in range(HALF // CHUNK):
+                lo = c * CHUNK
+                for a in range(PASSES):
+                    nc.tensor.matmul_mx(
+                        out=bank[b][:, h * HALF + lo : h * HALF + lo + CHUNK],
+                        lhsT=w_sb[:, a, 2 * P * b : 2 * P * (b + 1)].bitcast(FP4X4),
+                        lhsT_scale=wsc[:, a, P * b : P * (b + 1)],
+                        rhs=codes[a][h][:, lo : lo + CHUNK].bitcast(FP8X4),
+                        rhs_scale=xsc[a][h][:, lo : lo + CHUNK],
+                        start=(a == 0),
+                        stop=(a == PASSES - 1),
+                    )
+            cols = slice(h * HALF, (h + 1) * HALF)
+            nc.scalar.copy(y_sb[b][:, cols], bank[b][:, cols])
+
+        def scatter(b, h):
+            cols = slice(h * HALF, (h + 1) * HALF)
+            nc.vector.tensor_tensor(
+                window[b][:].indirect(list_out[:, h * OFF_COLS : (h + 1) * OFF_COLS]),
+                y_sb[b][:, cols],
+                wgo_sb[:, cols],
+                MULT,
+            )
+
+        for t in range(PACK):
+            gather(0, t, 0)
+            gather(0, t, 1)
+        interleave_scalar(0, 0, 0, HALF)
+        interleave_scalar(0, 1, 0, HALF)
+        gather(1, 0, 0)
+        gather(1, 0, 1)
+        gather(1, 1, 0)
+        quantize(0, 0, 0, HALF)
+        gather(1, 1, 1)
+        gather(1, 2, 0)
+        gather(1, 3, 0)
+        interleave_scalar(1, 0, 0, CHUNK)
+        gather(1, 2, 1)
+        interleave_vector(1, 0, CHUNK, HALF)
+        quantize(1, 0, 0, CHUNK)
+        quantize(1, 0, CHUNK, HALF)
+        gather(1, 3, 1)
+        quantize(0, 1, 0, HALF)
+        for b in range(BLOCKS):
+            multiply(b, 0)
+            scatter(b, 0)
+            if b == 1:
+                interleave_scalar(1, 1, 0, HALF)
+            if b == 3:
+                quantize(1, 1, 0, HALF)
+        for b in range(BLOCKS):
+            multiply(b, 1)
+            scatter(b, 1)
+            nc.sync.dma_start(out[P * b : P * (b + 1), :], window[b][:])

@@ -19,7 +19,7 @@ PASSES = K // (P * PACK)
 BLOCKS = M // P
 HALF = S // 2
 CHUNK = 128
-OFF_COLS = HALF // 16
+EARLY = 2
 
 
 def tile_list_hboth_none_kernel(tc, xT, w_words, w_scales, wgt, wgo, offs, offs2, out):
@@ -29,119 +29,111 @@ def tile_list_hboth_none_kernel(tc, xT, w_words, w_scales, wgt, wgo, offs, offs2
         list_out = held.tile([P, S // 16], U16, name="list_out")
         wgt_sb = held.tile([P, S], F32, name="wgt_sb")
         wgo_sb = held.tile([P, S], F32, name="wgo_sb")
-        w_sb = held.tile([P, PASSES, 2 * M], U8, name="w_sb", align_bytes=64)
+        w_early = held.tile([P, PASSES, 2 * P * EARLY], U8, name="w_early", align_bytes=64)
+        w_late = held.tile([P, PASSES, 2 * P * (BLOCKS - EARLY)], U8, name="w_late", align_bytes=64)
         wsc = held.tile([P, PASSES, M], U8, name="wsc", align_bytes=64)
         plane = [[held.tile([P, T], F32, name=f"plane{a}_{t}") for t in range(PACK)] for a in range(PASSES)]
-        picked = [[held.tile([P, PACK, HALF], F32, name=f"picked{a}_{h}") for h in range(2)] for a in range(PASSES)]
-        grouped = [[held.tile([P, HALF, PACK], BF16, name=f"grouped{a}_{h}", align_bytes=64) for h in range(2)] for a in range(PASSES)]
-        codes = [[held.tile([P, HALF], U32, name=f"codes{a}_{h}", align_bytes=64) for h in range(2)] for a in range(PASSES)]
-        xsc = [[held.tile([P, HALF], U8, name=f"xsc{a}_{h}", align_bytes=64) for h in range(2)] for a in range(PASSES)]
+        picked = [held.tile([P, PACK, S], F32, name=f"picked{a}") for a in range(PASSES)]
+        grouped0 = held.tile([P, S, PACK], BF16, name="grouped0", align_bytes=64)
+        grouped1_chunk = held.tile([P, CHUNK, PACK], BF16, name="grouped1_chunk", align_bytes=64)
+        grouped1_half = held.tile([P, HALF, PACK], BF16, name="grouped1_half", align_bytes=64)
+        codes = [held.tile([P, S], U32, name=f"codes{a}", align_bytes=64) for a in range(PASSES)]
+        xsc = [held.tile([P, S], U8, name=f"xsc{a}", align_bytes=64) for a in range(PASSES)]
         window = [held.tile([P, T], F32, name=f"window{b}") for b in range(BLOCKS)]
         y_sb = [held.tile([P, S], F32, name=f"y{b}") for b in range(BLOCKS)]
         bank = [psum.tile([P, S], F32, name=f"bank{b}") for b in range(BLOCKS)]
 
-        nc.gpsimd.memset(wsc[:].bitcast(I32), 0)
+        nc.vector.memset(wsc[:].bitcast(I32), 0)
         for b in range(BLOCKS):
-            nc.vector.memset(window[b][:] if b < 4 else window[b][:, 0:8], 0.0)
-        for b in range(4, BLOCKS):
             nc.gpsimd.memset(window[b][:], 0.0)
 
         rows = xT.rearrange("(a p t) n -> a t p n", p=P, t=PACK)
-        nc.sync.dma_start(list_in[:], offs)
+        words = w_words.bitcast(I32).rearrange("a p n -> p a n")
+        scale_rows = w_scales.bitcast(I32).rearrange("a (q r) n -> r q a n", r=4)
         nc.sync.dma_start(plane[0][0][:], rows[0, 0])
         nc.scalar.dma_start(wgt_sb[:, 0:HALF], wgt[:, 0:HALF])
+        nc.sync.dma_start(list_in[:], offs)
         nc.sync.dma_start(wgt_sb[:, HALF:S], wgt[:, HALF:S])
         for a in range(PASSES):
             for t in range(PACK):
                 if a + t > 0:
                     nc.sync.dma_start(plane[a][t][:], rows[a, t])
-        nc.sync.dma_start(w_sb[:].bitcast(I32), w_words.bitcast(I32).rearrange("a p n -> p a n"))
-        for q in range(4):
-            nc.sync.dma_start(
-                wsc[32 * q : 32 * q + 4].bitcast(I32),
-                w_scales.bitcast(I32)[:, 4 * q : 4 * q + 4, :].rearrange("a r n -> r a n"),
-            )
+        split = EARLY * P // 2
+        nc.sync.dma_start(w_early[:].bitcast(I32), words[:, :, 0:split])
+        for r in range(4):
+            nc.sync.dma_start(wsc[r:P:32].bitcast(I32), scale_rows[r])
         nc.sync.dma_start(list_out[:], offs2)
         nc.sync.dma_start(wgo_sb[:], wgo)
+        nc.sync.dma_start(w_late[:].bitcast(I32), words[:, :, split : M // 2])
 
-        def gather(a, t, h):
+        def gather(a, t, lo, hi):
             nc.vector.tensor_tensor(
-                picked[a][h][:, t, :],
-                plane[a][t][:].indirect(list_in[:, h * OFF_COLS : (h + 1) * OFF_COLS]),
-                wgt_sb[:, h * HALF : (h + 1) * HALF],
+                picked[a][:, t, lo:hi],
+                plane[a][t][:].indirect(list_in[:, lo // 16 : hi // 16]),
+                wgt_sb[:, lo:hi],
                 MULT,
             )
 
-        def views(a, h, lo, hi):
-            return grouped[a][h][:, lo:hi, :], picked[a][h][:, :, lo:hi].rearrange("p t c -> p c t")
-
-        def interleave_scalar(a, h, lo, hi):
-            dst, src = views(a, h, lo, hi)
-            nc.scalar.copy(dst, src)
-
-        def interleave_vector(a, h, lo, hi):
-            dst, src = views(a, h, lo, hi)
-            nc.vector.tensor_copy(dst, src)
-
-        def quantize(a, h, lo, hi):
-            nc.vector.quantize_mx(
-                out=codes[a][h][:, lo:hi].bitcast(FP8X4),
-                scales=xsc[a][h][:, lo:hi],
-                in_=grouped[a][h][:, lo:hi, :].rearrange("p c t -> p (c t)"),
+        def interleave(copy, dst, a, lo, hi):
+            copy(
+                dst[:].rearrange("p (c i) t -> p c t i", i=4),
+                picked[a][:, :, lo:hi].rearrange("p t (c i) -> p c t i", i=4),
             )
 
-        def multiply(b, h):
-            for c in range(HALF // CHUNK):
-                lo = c * CHUNK
+        def quantize(src, a, lo, hi):
+            nc.vector.quantize_mx(
+                out=codes[a][:, lo:hi].bitcast(FP8X4),
+                scales=xsc[a][:, lo:hi],
+                in_=src[:].rearrange("p c t -> p (c t)"),
+            )
+
+        def multiply(b, lo, hi):
+            w_sb, first = (w_early, b) if b < EARLY else (w_late, b - EARLY)
+            width = S if hi - lo == S else CHUNK
+            for c in range(lo, hi, width):
                 for a in range(PASSES):
                     nc.tensor.matmul_mx(
-                        out=bank[b][:, h * HALF + lo : h * HALF + lo + CHUNK],
-                        lhsT=w_sb[:, a, 2 * P * b : 2 * P * (b + 1)].bitcast(FP4X4),
+                        out=bank[b][:, c : c + width],
+                        lhsT=w_sb[:, a, 2 * P * first : 2 * P * (first + 1)].bitcast(FP4X4),
                         lhsT_scale=wsc[:, a, P * b : P * (b + 1)],
-                        rhs=codes[a][h][:, lo : lo + CHUNK].bitcast(FP8X4),
-                        rhs_scale=xsc[a][h][:, lo : lo + CHUNK],
+                        rhs=codes[a][:, c : c + width].bitcast(FP8X4),
+                        rhs_scale=xsc[a][:, c : c + width],
                         start=(a == 0),
                         stop=(a == PASSES - 1),
                     )
-            cols = slice(h * HALF, (h + 1) * HALF)
-            nc.scalar.copy(y_sb[b][:, cols], bank[b][:, cols])
 
-        def scatter(b, h):
-            cols = slice(h * HALF, (h + 1) * HALF)
+        def place(copy, b, lo, hi):
+            multiply(b, lo, hi)
+            copy(y_sb[b][:, lo:hi], bank[b][:, lo:hi])
             nc.vector.tensor_tensor(
-                window[b][:].indirect(list_out[:, h * OFF_COLS : (h + 1) * OFF_COLS]),
-                y_sb[b][:, cols],
-                wgo_sb[:, cols],
+                window[b][:].indirect(list_out[:, lo // 16 : hi // 16]),
+                y_sb[b][:, lo:hi],
+                wgo_sb[:, lo:hi],
                 MULT,
             )
+            if hi == S:
+                nc.sync.dma_start(out[P * b : P * (b + 1), :], window[b][:])
 
-        for t in range(PACK):
-            gather(0, t, 0)
-            gather(0, t, 1)
-        interleave_scalar(0, 0, 0, HALF)
-        interleave_scalar(0, 1, 0, HALF)
-        gather(1, 0, 0)
-        gather(1, 0, 1)
-        gather(1, 1, 0)
-        quantize(0, 0, 0, HALF)
-        gather(1, 1, 1)
-        gather(1, 2, 0)
-        gather(1, 3, 0)
-        interleave_scalar(1, 0, 0, CHUNK)
-        gather(1, 2, 1)
-        interleave_vector(1, 0, CHUNK, HALF)
-        quantize(1, 0, 0, CHUNK)
-        quantize(1, 0, CHUNK, HALF)
-        gather(1, 3, 1)
-        quantize(0, 1, 0, HALF)
-        for b in range(BLOCKS):
-            multiply(b, 0)
-            scatter(b, 0)
-            if b == 1:
-                interleave_scalar(1, 1, 0, HALF)
-            if b == 3:
-                quantize(1, 1, 0, HALF)
-        for b in range(BLOCKS):
-            multiply(b, 1)
-            scatter(b, 1)
-            nc.sync.dma_start(out[P * b : P * (b + 1), :], window[b][:])
+        gather(0, 0, 0, HALF)
+        gather(0, 0, HALF, S)
+        for t in range(1, PACK):
+            gather(0, t, 0, S)
+        interleave(nc.scalar.copy, grouped0, 0, 0, S)
+        for t in range(PACK - 1):
+            gather(1, t, 0, S)
+        quantize(grouped0, 0, 0, S)
+        gather(1, PACK - 1, 0, CHUNK)
+        gather(1, PACK - 1, CHUNK, S)
+        interleave(nc.scalar.copy, grouped1_chunk, 1, 0, CHUNK)
+        quantize(grouped1_chunk, 1, 0, CHUNK)
+        interleave(nc.scalar.copy, grouped1_half, 1, HALF, S)
+        interleave(nc.vector.tensor_copy, grouped1_chunk, 1, CHUNK, HALF)
+        quantize(grouped1_chunk, 1, CHUNK, HALF)
+        place(nc.vector.tensor_copy, 0, 0, CHUNK)
+        quantize(grouped1_half, 1, HALF, S)
+        place(nc.scalar.copy, 1, 0, HALF)
+        place(nc.scalar.copy, 2, 0, S)
+        place(nc.scalar.copy, 0, CHUNK, S)
+        place(nc.scalar.copy, 1, HALF, S)
+        for b in range(3, BLOCKS):
+            place(nc.scalar.copy, b, 0, S)

@@ -43,7 +43,7 @@ def tile_list_hboth_none_kernel(tc, xT, w_words, w_scales, wgt, wgo, offs, offs2
         y_sb = [held.tile([P, S], F32, name=f"y{b}") for b in range(BLOCKS)]
         bank = [psum.tile([P, S], F32, name=f"bank{b}") for b in range(BLOCKS)]
 
-        nc.vector.memset(wsc[:].bitcast(I32), 0)
+        nc.gpsimd.memset(wsc[:].bitcast(I32), 0)
         for b in range(BLOCKS):
             nc.gpsimd.memset(window[b][:], 0.0)
 

@@ -20,6 +20,7 @@ BLOCKS = M // P
 HALF = S // 2
 CHUNK = 128
 EARLY = 2
+PIECES = ((0, CHUNK), (CHUNK, HALF), (HALF, S))
 
 
 def tile_list_hboth_none_kernel(tc, xT, w_words, w_scales, wgt, wgo, offs, offs2, out):
@@ -34,11 +35,11 @@ def tile_list_hboth_none_kernel(tc, xT, w_words, w_scales, wgt, wgo, offs, offs2
         wsc = held.tile([P, PASSES, M], U8, name="wsc", align_bytes=64)
         plane = [[held.tile([P, T], F32, name=f"plane{a}_{t}") for t in range(PACK)] for a in range(PASSES)]
         picked = [held.tile([P, PACK, S], F32, name=f"picked{a}") for a in range(PASSES)]
-        grouped0 = held.tile([P, S, PACK], BF16, name="grouped0", align_bytes=64)
-        grouped1_chunk = held.tile([P, CHUNK, PACK], BF16, name="grouped1_chunk", align_bytes=64)
-        grouped1_half = held.tile([P, HALF, PACK], BF16, name="grouped1_half", align_bytes=64)
-        codes = [held.tile([P, S], U32, name=f"codes{a}", align_bytes=64) for a in range(PASSES)]
-        xsc = [held.tile([P, S], U8, name=f"xsc{a}", align_bytes=64) for a in range(PASSES)]
+        grouped, codes, xsc = {}, {}, {}
+        for lo, hi in PIECES:
+            grouped[lo] = held.tile([P, PASSES * (hi - lo) * PACK], BF16, name=f"grouped{lo}", align_bytes=64)
+            codes[lo] = held.tile([P, PASSES * (hi - lo)], U32, name=f"codes{lo}", align_bytes=64)
+            xsc[lo] = held.tile([P, PASSES * (hi - lo)], U8, name=f"xsc{lo}", align_bytes=64)
         window = [held.tile([P, T], F32, name=f"window{b}") for b in range(BLOCKS)]
         y_sb = [held.tile([P, S], F32, name=f"y{b}") for b in range(BLOCKS)]
         bank = [psum.tile([P, S], F32, name=f"bank{b}") for b in range(BLOCKS)]
@@ -51,9 +52,9 @@ def tile_list_hboth_none_kernel(tc, xT, w_words, w_scales, wgt, wgo, offs, offs2
         words = w_words.bitcast(I32).rearrange("a p n -> p a n")
         scale_rows = w_scales.bitcast(I32).rearrange("a (q r) n -> r q a n", r=4)
         nc.sync.dma_start(plane[0][0][:], rows[0, 0])
-        nc.scalar.dma_start(wgt_sb[:, 0:HALF], wgt[:, 0:HALF])
+        nc.scalar.dma_start(wgt_sb[:, 0:CHUNK], wgt[:, 0:CHUNK])
         nc.sync.dma_start(list_in[:], offs)
-        nc.sync.dma_start(wgt_sb[:, HALF:S], wgt[:, HALF:S])
+        nc.sync.dma_start(wgt_sb[:, CHUNK:S], wgt[:, CHUNK:S])
         for a in range(PASSES):
             for t in range(PACK):
                 if a + t > 0:
@@ -74,36 +75,34 @@ def tile_list_hboth_none_kernel(tc, xT, w_words, w_scales, wgt, wgo, offs, offs2
                 MULT,
             )
 
-        def interleave(copy, dst, a, lo, hi):
-            copy(
-                dst[:].rearrange("p (c i) t -> p c t i", i=4),
+        def interleave(a, lo, hi):
+            size = (hi - lo) * PACK
+            nc.scalar.copy(
+                grouped[lo][:, a * size : (a + 1) * size].rearrange("p (c i t) -> p c t i", i=4, t=PACK),
                 picked[a][:, :, lo:hi].rearrange("p t (c i) -> p c t i", i=4),
             )
 
-        def quantize(src, a, lo, hi):
-            nc.vector.quantize_mx(
-                out=codes[a][:, lo:hi].bitcast(FP8X4),
-                scales=xsc[a][:, lo:hi],
-                in_=src[:].rearrange("p c t -> p (c t)"),
-            )
+        def quantize(lo):
+            nc.vector.quantize_mx(out=codes[lo][:].bitcast(FP8X4), scales=xsc[lo][:], in_=grouped[lo][:])
 
-        def multiply(b, lo, hi):
+        def multiply(b, c):
             w_sb, first = (w_early, b) if b < EARLY else (w_late, b - EARLY)
-            width = S if hi - lo == S else CHUNK
-            for c in range(lo, hi, width):
-                for a in range(PASSES):
-                    nc.tensor.matmul_mx(
-                        out=bank[b][:, c : c + width],
-                        lhsT=w_sb[:, a, 2 * P * first : 2 * P * (first + 1)].bitcast(FP4X4),
-                        lhsT_scale=wsc[:, a, P * b : P * (b + 1)],
-                        rhs=codes[a][:, c : c + width].bitcast(FP8X4),
-                        rhs_scale=xsc[a][:, c : c + width],
-                        start=(a == 0),
-                        stop=(a == PASSES - 1),
-                    )
+            lo, hi = [piece for piece in PIECES if piece[0] <= c < piece[1]][0]
+            for a in range(PASSES):
+                at = a * (hi - lo) + c - lo
+                nc.tensor.matmul_mx(
+                    out=bank[b][:, c : c + CHUNK],
+                    lhsT=w_sb[:, a, 2 * P * first : 2 * P * (first + 1)].bitcast(FP4X4),
+                    lhsT_scale=wsc[:, a, P * b : P * (b + 1)],
+                    rhs=codes[lo][:, at : at + CHUNK].bitcast(FP8X4),
+                    rhs_scale=xsc[lo][:, at : at + CHUNK],
+                    start=(a == 0),
+                    stop=(a == PASSES - 1),
+                )
 
         def place(copy, b, lo, hi):
-            multiply(b, lo, hi)
+            for c in range(lo, hi, CHUNK):
+                multiply(b, c)
             copy(y_sb[b][:, lo:hi], bank[b][:, lo:hi])
             nc.vector.tensor_tensor(
                 window[b][:].indirect(list_out[:, lo // 16 : hi // 16]),
@@ -114,23 +113,22 @@ def tile_list_hboth_none_kernel(tc, xT, w_words, w_scales, wgt, wgo, offs, offs2
             if hi == S:
                 nc.sync.dma_start(out[P * b : P * (b + 1), :], window[b][:])
 
-        gather(0, 0, 0, HALF)
-        gather(0, 0, HALF, S)
+        gather(0, 0, 0, CHUNK)
+        gather(0, 0, CHUNK, S)
         for t in range(1, PACK):
             gather(0, t, 0, S)
-        interleave(nc.scalar.copy, grouped0, 0, 0, S)
+        for lo, hi in PIECES:
+            interleave(0, lo, hi)
         for t in range(PACK - 1):
             gather(1, t, 0, S)
-        quantize(grouped0, 0, 0, S)
         gather(1, PACK - 1, 0, CHUNK)
         gather(1, PACK - 1, CHUNK, S)
-        interleave(nc.scalar.copy, grouped1_chunk, 1, 0, CHUNK)
-        quantize(grouped1_chunk, 1, 0, CHUNK)
-        interleave(nc.scalar.copy, grouped1_half, 1, HALF, S)
-        interleave(nc.vector.tensor_copy, grouped1_chunk, 1, CHUNK, HALF)
-        quantize(grouped1_chunk, 1, CHUNK, HALF)
+        for lo, hi in PIECES:
+            interleave(1, lo, hi)
+        quantize(0)
+        quantize(CHUNK)
         place(nc.vector.tensor_copy, 0, 0, CHUNK)
-        quantize(grouped1_half, 1, HALF, S)
+        quantize(HALF)
         place(nc.scalar.copy, 1, 0, HALF)
         place(nc.scalar.copy, 2, 0, S)
         place(nc.scalar.copy, 0, CHUNK, S)

@@ -28,16 +28,22 @@ def tile_list_hboth_none_kernel(tc, xT, w_words, w_scales, wgt, wgo, offs, offs2
     with tc.tile_pool(name="held", bufs=1) as held, tc.psum_pool(name="psum", bufs=1) as psum:
         list_in = held.tile([P, S // 16], U16, name="list_in")
         list_out = held.tile([P, S // 16], U16, name="list_out")
-        wgt_sb = held.tile([P, S], F32, name="wgt_sb")
         wgo_sb = held.tile([P, S], F32, name="wgo_sb")
         w_early = held.tile([P, PASSES, 2 * P * EARLY], U8, name="w_early", align_bytes=64)
         w_late = held.tile([P, PASSES, 2 * P * (BLOCKS - EARLY)], U8, name="w_late", align_bytes=64)
         wsc = held.tile([P, PASSES, M], U8, name="wsc", align_bytes=64)
         plane = [[held.tile([P, T], F32, name=f"plane{a}_{t}") for t in range(PACK)] for a in range(PASSES)]
-        picked = [held.tile([P, PACK, S], F32, name=f"picked{a}") for a in range(PASSES)]
-        grouped, codes, xsc = {}, {}, {}
+        picked0 = held.tile([P, PACK, S], F32, name="picked0")
+        shared = held.tile([P, 8 * S], F32, name="shared", align_bytes=64)
+        wgt_sb = held.tile([P, S], F32, name="wgt_sb")
+        grouped_half = held.tile([P, PASSES * HALF * PACK], BF16, name="grouped_half", align_bytes=64)
+        grouped = {
+            0: shared[:, 4 * S : 5 * S].bitcast(BF16),
+            CHUNK: shared[:, 5 * S : 6 * S].bitcast(BF16),
+            HALF: grouped_half[:],
+        }
+        codes, xsc = {}, {}
         for lo, hi in PIECES:
-            grouped[lo] = held.tile([P, PASSES * (hi - lo) * PACK], BF16, name=f"grouped{lo}", align_bytes=64)
             codes[lo] = held.tile([P, PASSES * (hi - lo)], U32, name=f"codes{lo}", align_bytes=64)
             xsc[lo] = held.tile([P, PASSES * (hi - lo)], U8, name=f"xsc{lo}", align_bytes=64)
         window = [held.tile([P, T], F32, name=f"window{b}") for b in range(BLOCKS)]
@@ -67,23 +73,29 @@ def tile_list_hboth_none_kernel(tc, xT, w_words, w_scales, wgt, wgo, offs, offs2
         nc.sync.dma_start(wgo_sb[:], wgo)
         nc.sync.dma_start(w_late[:].bitcast(I32), words[:, :, split : M // 2])
 
+        def picked(a, lo, hi):
+            if a == 0:
+                return picked0[:, :, lo:hi].rearrange("p (u v) c -> p u v c", u=2)
+            pair = 2 * S if lo < HALF else 4 * S
+            both = shared[:, 0 : 2 * pair].rearrange("p (u x) -> p u x", u=2)
+            return both[:, :, 0 : 2 * S].rearrange("p u (v c) -> p u v c", v=2)[:, :, :, lo:hi]
+
         def gather(a, t, lo, hi):
             nc.vector.tensor_tensor(
-                picked[a][:, t, lo:hi],
+                picked(a, lo, hi)[:, t // 2, t % 2, :],
                 plane[a][t][:].indirect(list_in[:, lo // 16 : hi // 16]),
                 wgt_sb[:, lo:hi],
                 MULT,
             )
 
-        def interleave(a, lo, hi):
+        def interleave(a, lo, hi, pairs=slice(0, 2)):
             size = (hi - lo) * PACK
-            nc.scalar.copy(
-                grouped[lo][:, a * size : (a + 1) * size].rearrange("p (c i t) -> p c t i", i=4, t=PACK),
-                picked[a][:, :, lo:hi].rearrange("p t (c i) -> p c t i", i=4),
-            )
+            dst = grouped[lo][:, a * size : (a + 1) * size].rearrange("p (c i u v) -> p c u v i", i=4, u=2, v=2)
+            src = picked(a, lo, hi).rearrange("p u v (c i) -> p c u v i", i=4)
+            nc.scalar.copy(dst[:, :, pairs], src[:, :, pairs])
 
         def quantize(lo):
-            nc.vector.quantize_mx(out=codes[lo][:].bitcast(FP8X4), scales=xsc[lo][:], in_=grouped[lo][:])
+            nc.vector.quantize_mx(out=codes[lo][:].bitcast(FP8X4), scales=xsc[lo][:], in_=grouped[lo])
 
         def multiply(b, c):
             w_sb, first = (w_early, b) if b < EARLY else (w_late, b - EARLY)
@@ -100,13 +112,13 @@ def tile_list_hboth_none_kernel(tc, xT, w_words, w_scales, wgt, wgo, offs, offs2
                     stop=(a == PASSES - 1),
                 )
 
-        def place(copy, b, lo, hi):
+        def place(b, lo, hi, y):
             for c in range(lo, hi, CHUNK):
                 multiply(b, c)
-            copy(y_sb[b][:, lo:hi], bank[b][:, lo:hi])
+            nc.scalar.copy(y, bank[b][:, lo:hi])
             nc.vector.tensor_tensor(
                 window[b][:].indirect(list_out[:, lo // 16 : hi // 16]),
-                y_sb[b][:, lo:hi],
+                y,
                 wgo_sb[:, lo:hi],
                 MULT,
             )
@@ -119,19 +131,26 @@ def tile_list_hboth_none_kernel(tc, xT, w_words, w_scales, wgt, wgo, offs, offs2
             gather(0, t, 0, S)
         for lo, hi in PIECES:
             interleave(0, lo, hi)
-        for t in range(PACK - 1):
-            gather(1, t, 0, S)
-        gather(1, PACK - 1, 0, CHUNK)
-        gather(1, PACK - 1, CHUNK, S)
-        for lo, hi in PIECES:
-            interleave(1, lo, hi)
+        gather(1, 0, 0, S)
+        gather(1, 1, 0, S)
+        interleave(1, 0, CHUNK, slice(0, 1))
+        gather(1, 2, 0, HALF)
+        gather(1, 3, 0, CHUNK)
+        gather(1, 3, CHUNK, HALF)
+        interleave(1, 0, CHUNK, slice(1, 2))
+        interleave(1, CHUNK, HALF)
         quantize(0)
+        gather(1, 2, HALF, S)
         quantize(CHUNK)
-        place(nc.vector.tensor_copy, 0, 0, CHUNK)
+        gather(1, 3, HALF, S)
+        place(0, 0, CHUNK, grouped[HALF][:, HALF * PACK : HALF * PACK + 2 * CHUNK].bitcast(F32))
+        place(1, 0, HALF, y_sb[1][:, 0:HALF])
+        interleave(1, HALF, S)
         quantize(HALF)
-        place(nc.scalar.copy, 1, 0, HALF)
-        place(nc.scalar.copy, 2, 0, S)
-        place(nc.scalar.copy, 0, CHUNK, S)
-        place(nc.scalar.copy, 1, HALF, S)
-        for b in range(3, BLOCKS):
-            place(nc.scalar.copy, b, 0, S)
+        place(2, 0, HALF, y_sb[2][:, 0:HALF])
+        place(3, 0, S, y_sb[3][:])
+        place(0, CHUNK, S, y_sb[0][:, CHUNK:S])
+        place(1, HALF, S, y_sb[1][:, HALF:S])
+        place(2, HALF, S, y_sb[2][:, HALF:S])
+        for b in range(4, BLOCKS):
+            place(b, 0, S, y_sb[b][:])

@@ -21,6 +21,7 @@ HALF = S // 2
 CHUNK = 128
 EARLY = 2
 PIECES = ((0, CHUNK), (CHUNK, HALF), (HALF, S))
+WINDOWS = 4
 
 
 def tile_list_hboth_none_kernel(tc, xT, w_words, w_scales, wgt, wgo, offs, offs2, out):
@@ -46,13 +47,14 @@ def tile_list_hboth_none_kernel(tc, xT, w_words, w_scales, wgt, wgo, offs, offs2
         for lo, hi in PIECES:
             codes[lo] = held.tile([P, PASSES * (hi - lo)], U32, name=f"codes{lo}", align_bytes=64)
             xsc[lo] = held.tile([P, PASSES * (hi - lo)], U8, name=f"xsc{lo}", align_bytes=64)
-        window = [held.tile([P, T], F32, name=f"window{b}") for b in range(BLOCKS)]
+        zeroed = [held.tile([P, T], F32, name=f"window{i}") for i in range(WINDOWS)]
+        window = zeroed + [zeroed[i] for i in (3, 0, 1, 2)]
         y_sb = [held.tile([P, S], F32, name=f"y{b}") for b in range(BLOCKS)]
         bank = [psum.tile([P, S], F32, name=f"bank{b}") for b in range(BLOCKS)]
 
-        nc.gpsimd.memset(wsc[:].bitcast(I32), 0)
-        for b in range(BLOCKS):
-            nc.gpsimd.memset(window[b][:], 0.0)
+        nc.vector.memset(wsc[:].bitcast(I32), 0)
+        for tile in zeroed:
+            nc.vector.memset(tile[:], 0.0)
 
         rows = xT.rearrange("(a p t) n -> a t p n", p=P, t=PACK)
         words = w_words.bitcast(I32).rearrange("a p n -> p a n")

@@ -33,20 +33,23 @@ def tile_list_hboth_none_kernel(tc, xT, w_words, w_scales, wgt, wgo, offs, offs2
         w_early = held.tile([P, PASSES, 2 * P * EARLY], U8, name="w_early", align_bytes=64)
         w_late = held.tile([P, PASSES, 2 * P * (BLOCKS - EARLY)], U8, name="w_late", align_bytes=64)
         wsc = held.tile([P, PASSES, M], U8, name="wsc", align_bytes=64)
-        plane = [[held.tile([P, T], F32, name=f"plane{a}_{t}") for t in range(PACK)] for a in range(PASSES)]
+        plane = [[held.tile([P, T], F32, name=f"plane{a}_{t}", align_bytes=64) for t in range(PACK)] for a in range(PASSES)]
         picked0 = held.tile([P, PACK, S], F32, name="picked0")
         shared = held.tile([P, 8 * S], F32, name="shared", align_bytes=64)
-        wgt_sb = held.tile([P, S], F32, name="wgt_sb")
+        wgt_sb = shared[:, 5 * S - CHUNK : 6 * S - CHUNK]
+        grouped_chunk = held.tile([P, PASSES * CHUNK * PACK], BF16, name="grouped_chunk", align_bytes=64)
         grouped_half = held.tile([P, PASSES * HALF * PACK], BF16, name="grouped_half", align_bytes=64)
         grouped = {
-            0: shared[:, 4 * S : 5 * S].bitcast(BF16),
-            CHUNK: shared[:, 5 * S : 6 * S].bitcast(BF16),
+            0: shared[:, 6 * S : 7 * S].bitcast(BF16),
+            CHUNK: grouped_chunk[:],
             HALF: grouped_half[:],
         }
         codes, xsc = {}, {}
         for lo, hi in PIECES:
-            codes[lo] = held.tile([P, PASSES * (hi - lo)], U32, name=f"codes{lo}", align_bytes=64)
+            both = held.tile([P, PASSES * (hi - lo)], U32, name=f"codes{lo}", align_bytes=64)
+            codes[lo] = [both[:, a * (hi - lo) : (a + 1) * (hi - lo)] for a in range(PASSES)]
             xsc[lo] = held.tile([P, PASSES * (hi - lo)], U8, name=f"xsc{lo}", align_bytes=64)
+            codes[lo].append(both[:])
         zeroed = [held.tile([P, T], F32, name=f"window{i}") for i in range(WINDOWS)]
         window = zeroed + [zeroed[i] for i in (3, 0, 1, 2)]
         y_sb = [held.tile([P, S], F32, name=f"y{b}") for b in range(BLOCKS)]
@@ -78,9 +81,9 @@ def tile_list_hboth_none_kernel(tc, xT, w_words, w_scales, wgt, wgo, offs, offs2
         def picked(a, lo, hi):
             if a == 0:
                 return picked0[:, :, lo:hi].rearrange("p (u v) c -> p u v c", u=2)
-            pair = 2 * S if lo < HALF else 4 * S
-            both = shared[:, 0 : 2 * pair].rearrange("p (u x) -> p u x", u=2)
-            return both[:, :, 0 : 2 * S].rearrange("p u (v c) -> p u v c", v=2)[:, :, :, lo:hi]
+            if lo < HALF:
+                return shared[:, 0 : 4 * S].rearrange("p (v u c) -> p u v c", v=2, u=2)[:, :, :, lo:hi]
+            return shared[:].rearrange("p (u v c) -> p u v c", u=2, v=2)[:, :, :, lo:hi]
 
         def gather(a, t, lo, hi):
             nc.vector.tensor_tensor(
@@ -97,21 +100,30 @@ def tile_list_hboth_none_kernel(tc, xT, w_words, w_scales, wgt, wgo, offs, offs2
             nc.scalar.copy(dst[:, :, pairs], src[:, :, pairs])
 
         def quantize(lo):
-            nc.vector.quantize_mx(out=codes[lo][:].bitcast(FP8X4), scales=xsc[lo][:], in_=grouped[lo])
+            nc.vector.quantize_mx(out=codes[lo][PASSES].bitcast(FP8X4), scales=xsc[lo][:], in_=grouped[lo])
+
+        def quantize_pass(a, lo, hi):
+            width = hi - lo
+            nc.vector.quantize_mx(
+                out=codes[lo][a].bitcast(FP8X4),
+                scales=xsc[lo][:, a * width : (a + 1) * width],
+                in_=grouped[lo][:, a * width * PACK : (a + 1) * width * PACK],
+            )
 
         def multiply(b, c):
             w_sb, first = (w_early, b) if b < EARLY else (w_late, b - EARLY)
             lo, hi = [piece for piece in PIECES if piece[0] <= c < piece[1]][0]
-            for a in range(PASSES):
+            order = range(PASSES) if b < EARLY else range(PASSES - 1, -1, -1)
+            for a in order:
                 at = a * (hi - lo) + c - lo
                 nc.tensor.matmul_mx(
                     out=bank[b][:, c : c + CHUNK],
                     lhsT=w_sb[:, a, 2 * P * first : 2 * P * (first + 1)].bitcast(FP4X4),
                     lhsT_scale=wsc[:, a, P * b : P * (b + 1)],
-                    rhs=codes[lo][:, at : at + CHUNK].bitcast(FP8X4),
+                    rhs=codes[lo][a][:, c - lo : c - lo + CHUNK].bitcast(FP8X4),
                     rhs_scale=xsc[lo][:, at : at + CHUNK],
-                    start=(a == 0),
-                    stop=(a == PASSES - 1),
+                    start=(a == order[0]),
+                    stop=(a == order[-1]),
                 )
 
         def place(b, lo, hi, y):
@@ -134,21 +146,25 @@ def tile_list_hboth_none_kernel(tc, xT, w_words, w_scales, wgt, wgo, offs, offs2
         for lo, hi in PIECES:
             interleave(0, lo, hi)
         gather(1, 0, 0, S)
+        quantize_pass(0, 0, CHUNK)
         gather(1, 1, 0, S)
         interleave(1, 0, CHUNK, slice(0, 1))
         gather(1, 2, 0, HALF)
         gather(1, 3, 0, CHUNK)
         gather(1, 3, CHUNK, HALF)
+        gather(1, 2, HALF, S)
         interleave(1, 0, CHUNK, slice(1, 2))
         interleave(1, CHUNK, HALF)
-        quantize(0)
-        gather(1, 2, HALF, S)
-        quantize(CHUNK)
+        quantize_pass(1, 0, CHUNK)
         gather(1, 3, HALF, S)
+        quantize(CHUNK)
+        late = held.tile([P, HALF], U32, name="codes_late", tag="plane1_3", align_bytes=64)
+        codes[HALF][0] = late[:]
+        quantize_pass(0, HALF, S)
         place(0, 0, CHUNK, grouped[HALF][:, HALF * PACK : HALF * PACK + 2 * CHUNK].bitcast(F32))
         place(1, 0, HALF, y_sb[1][:, 0:HALF])
         interleave(1, HALF, S)
-        quantize(HALF)
+        quantize_pass(1, HALF, S)
         place(2, 0, HALF, y_sb[2][:, 0:HALF])
         place(3, 0, S, y_sb[3][:])
         place(0, CHUNK, S, y_sb[0][:, CHUNK:S])

@@ -136,8 +136,11 @@ def tile_list_hboth_none_kernel(tc, xT, w_words, w_scales, wgt, wgo, offs, offs2
                 wgo_sb[:, lo:hi],
                 MULT,
             )
-            if hi == S:
+            if hi == S and b < BLOCKS - 1:
                 nc.sync.dma_start(out[P * b : P * (b + 1), :], window[b][:])
+            elif hi == S:
+                nc.sync.dma_start(out[P * b : P * (b + 1), 0 : T // 2], window[b][:, 0 : T // 2])
+                nc.scalar.dma_start(out[P * b : P * (b + 1), T // 2 : T], window[b][:, T // 2 : T])
 
         gather(0, 0, 0, CHUNK)
         gather(0, 0, CHUNK, S)

@@ -55,9 +55,9 @@ def tile_list_hboth_none_kernel(tc, xT, w_words, w_scales, wgt, wgo, offs, offs2
         y_sb = [held.tile([P, S], F32, name=f"y{b}") for b in range(BLOCKS)]
         bank = [psum.tile([P, S], F32, name=f"bank{b}") for b in range(BLOCKS)]
 
-        nc.vector.memset(wsc[:].bitcast(I32), 0)
+        nc.gpsimd.memset(wsc[:].bitcast(I32), 0)
         for tile in zeroed:
-            nc.vector.memset(tile[:], 0.0)
+            nc.gpsimd.memset(tile[:], 0.0)
 
         rows = xT.rearrange("(a p t) n -> a t p n", p=P, t=PACK)
         words = w_words.bitcast(I32).rearrange("a p n -> p a n")

@@ -19,7 +19,7 @@ PASSES = K // (P * PACK)
 BLOCKS = M // P
 HALF = S // 2
 CHUNK = 128
-EARLY = 2
+EARLY = 4
 PIECES = ((0, CHUNK), (CHUNK, HALF), (HALF, S))
 WINDOWS = 4
 
@@ -35,14 +35,15 @@ def tile_list_hboth_none_kernel(tc, xT, w_words, w_scales, wgt, wgo, offs, offs2
         wsc = held.tile([P, PASSES, M], U8, name="wsc", align_bytes=64)
         plane = [[held.tile([P, T], F32, name=f"plane{a}_{t}", align_bytes=64) for t in range(PACK)] for a in range(PASSES)]
         picked0 = held.tile([P, PACK, S], F32, name="picked0")
-        shared = held.tile([P, 8 * S], F32, name="shared", align_bytes=64)
-        wgt_sb = shared[:, 5 * S - CHUNK : 6 * S - CHUNK]
+        picked1 = held.tile([P, PACK * S], F32, name="picked1", align_bytes=64)
+        wgt_sb = held.tile([P, S], F32, name="wgt_sb")
+        grouped_first = [held.tile([P, CHUNK * PACK], BF16, name=f"grouped_first{a}", align_bytes=64) for a in range(PASSES)]
         grouped_chunk = held.tile([P, PASSES * CHUNK * PACK], BF16, name="grouped_chunk", align_bytes=64)
         grouped_half = held.tile([P, PASSES * HALF * PACK], BF16, name="grouped_half", align_bytes=64)
         grouped = {
-            0: shared[:, 6 * S : 7 * S].bitcast(BF16),
-            CHUNK: grouped_chunk[:],
-            HALF: grouped_half[:],
+            0: [tile[:] for tile in grouped_first],
+            CHUNK: [grouped_chunk[:, a * CHUNK * PACK : (a + 1) * CHUNK * PACK] for a in range(PASSES)],
+            HALF: [grouped_half[:, a * HALF * PACK : (a + 1) * HALF * PACK] for a in range(PASSES)],
         }
         codes, xsc = {}, {}
         for lo, hi in PIECES:
@@ -51,13 +52,13 @@ def tile_list_hboth_none_kernel(tc, xT, w_words, w_scales, wgt, wgo, offs, offs2
             xsc[lo] = held.tile([P, PASSES * (hi - lo)], U8, name=f"xsc{lo}", align_bytes=64)
             codes[lo].append(both[:])
         zeroed = [held.tile([P, T], F32, name=f"window{i}") for i in range(WINDOWS)]
-        window = zeroed + [zeroed[i] for i in (3, 0, 1, 2)]
+        window = [zeroed[b % WINDOWS] for b in range(BLOCKS)]
         y_sb = [held.tile([P, S], F32, name=f"y{b}") for b in range(BLOCKS)]
         bank = [psum.tile([P, S], F32, name=f"bank{b}") for b in range(BLOCKS)]
 
-        nc.gpsimd.memset(wsc[:].bitcast(I32), 0)
+        nc.vector.memset(wsc[:].bitcast(I32), 0)
         for tile in zeroed:
-            nc.gpsimd.memset(tile[:], 0.0)
+            nc.vector.memset(tile[:], 0.0)
 
         rows = xT.rearrange("(a p t) n -> a t p n", p=P, t=PACK)
         words = w_words.bitcast(I32).rearrange("a p n -> p a n")
@@ -81,43 +82,42 @@ def tile_list_hboth_none_kernel(tc, xT, w_words, w_scales, wgt, wgo, offs, offs2
         def picked(a, lo, hi):
             if a == 0:
                 return picked0[:, :, lo:hi].rearrange("p (u v) c -> p u v c", u=2)
-            if lo < HALF:
-                return shared[:, 0 : 4 * S].rearrange("p (v u c) -> p u v c", v=2, u=2)[:, :, :, lo:hi]
-            return shared[:].rearrange("p (u v c) -> p u v c", u=2, v=2)[:, :, :, lo:hi]
+            return picked1[:].rearrange("p (u v c) -> p u v c", u=2, v=2)[:, :, :, lo:hi]
 
-        def gather(a, t, lo, hi):
+        last_pair = picked1[:, 2 * S : 3 * S].rearrange("p (v c) -> p v c", v=2)[:, :, 0:CHUNK]
+
+        def gather(a, t, lo, hi, dst=None):
             nc.vector.tensor_tensor(
-                picked(a, lo, hi)[:, t // 2, t % 2, :],
+                picked(a, lo, hi)[:, t // 2, t % 2, :] if dst is None else dst,
                 plane[a][t][:].indirect(list_in[:, lo // 16 : hi // 16]),
                 wgt_sb[:, lo:hi],
                 MULT,
             )
 
         def interleave(a, lo, hi, pairs=slice(0, 2)):
-            size = (hi - lo) * PACK
-            dst = grouped[lo][:, a * size : (a + 1) * size].rearrange("p (c i u v) -> p c u v i", i=4, u=2, v=2)
+            dst = grouped[lo][a].rearrange("p (c i u v) -> p c u v i", i=4, u=2, v=2)
             src = picked(a, lo, hi).rearrange("p u v (c i) -> p c u v i", i=4)
             nc.scalar.copy(dst[:, :, pairs], src[:, :, pairs])
 
-        def quantize(lo):
-            nc.vector.quantize_mx(out=codes[lo][PASSES].bitcast(FP8X4), scales=xsc[lo][:], in_=grouped[lo])
+        def quantize_chunk():
+            nc.vector.quantize_mx(out=codes[CHUNK][PASSES].bitcast(FP8X4), scales=xsc[CHUNK][:], in_=grouped_chunk[:])
 
         def quantize_pass(a, lo, hi):
             width = hi - lo
             nc.vector.quantize_mx(
                 out=codes[lo][a].bitcast(FP8X4),
                 scales=xsc[lo][:, a * width : (a + 1) * width],
-                in_=grouped[lo][:, a * width * PACK : (a + 1) * width * PACK],
+                in_=grouped[lo][a],
             )
 
-        def multiply(b, c):
+        def multiply(b, c, into):
             w_sb, first = (w_early, b) if b < EARLY else (w_late, b - EARLY)
             lo, hi = [piece for piece in PIECES if piece[0] <= c < piece[1]][0]
-            order = range(PASSES) if b < EARLY else range(PASSES - 1, -1, -1)
+            order = range(PASSES) if b < 2 else range(PASSES - 1, -1, -1)
             for a in order:
                 at = a * (hi - lo) + c - lo
                 nc.tensor.matmul_mx(
-                    out=bank[b][:, c : c + CHUNK],
+                    out=into,
                     lhsT=w_sb[:, a, 2 * P * first : 2 * P * (first + 1)].bitcast(FP4X4),
                     lhsT_scale=wsc[:, a, P * b : P * (b + 1)],
                     rhs=codes[lo][a][:, c - lo : c - lo + CHUNK].bitcast(FP8X4),
@@ -126,18 +126,22 @@ def tile_list_hboth_none_kernel(tc, xT, w_words, w_scales, wgt, wgo, offs, offs2
                     stop=(a == order[-1]),
                 )
 
-        def place(b, lo, hi, y):
+        def place(b, lo, hi, y, acc=None):
+            acc = bank[b] if acc is None else acc
             for c in range(lo, hi, CHUNK):
-                multiply(b, c)
-            nc.scalar.copy(y, bank[b][:, lo:hi])
+                multiply(b, c, acc[:, c : c + CHUNK])
+            nc.scalar.copy(y, acc[:, lo:hi])
             nc.vector.tensor_tensor(
                 window[b][:].indirect(list_out[:, lo // 16 : hi // 16]),
                 y,
                 wgo_sb[:, lo:hi],
                 MULT,
             )
-            if hi == S and b < BLOCKS - 1:
+            if hi == S and EARLY <= b < BLOCKS - 1:
                 nc.sync.dma_start(out[P * b : P * (b + 1), :], window[b][:])
+            elif hi == S and b < EARLY:
+                nc.sync.dma_start(out[P * b : P * (b + 1), 0 : T // 2], window[b][:, 0 : T // 2])
+                nc.sync.dma_start(out[P * b : P * (b + 1), T // 2 : T], window[b][:, T // 2 : T])
             elif hi == S:
                 nc.sync.dma_start(out[P * b : P * (b + 1), 0 : T // 2], window[b][:, 0 : T // 2])
                 nc.scalar.dma_start(out[P * b : P * (b + 1), T // 2 : T], window[b][:, T // 2 : T])
@@ -152,26 +156,29 @@ def tile_list_hboth_none_kernel(tc, xT, w_words, w_scales, wgt, wgo, offs, offs2
         quantize_pass(0, 0, CHUNK)
         gather(1, 1, 0, S)
         interleave(1, 0, CHUNK, slice(0, 1))
+        interleave(1, CHUNK, HALF, slice(0, 1))
         gather(1, 2, 0, HALF)
-        gather(1, 3, 0, CHUNK)
-        gather(1, 3, CHUNK, HALF)
-        gather(1, 2, HALF, S)
-        interleave(1, 0, CHUNK, slice(1, 2))
-        interleave(1, CHUNK, HALF)
+        gather(1, 3, 0, CHUNK, last_pair[:, 1, :])
+        gather(1, 3, CHUNK, S)
+        nc.scalar.copy(
+            grouped[0][1].rearrange("p (c i u v) -> p c u v i", i=4, u=2, v=2)[:, :, 1],
+            last_pair.rearrange("p v (c i) -> p c v i", i=4),
+        )
+        interleave(1, CHUNK, HALF, slice(1, 2))
         quantize_pass(1, 0, CHUNK)
-        gather(1, 3, HALF, S)
-        quantize(CHUNK)
-        late = held.tile([P, HALF], U32, name="codes_late", tag="plane1_3", align_bytes=64)
+        gather(1, 2, HALF, S)
+        late = held.tile([P, HALF], U32, name="codes_late", tag="grouped_first1", align_bytes=64)
         codes[HALF][0] = late[:]
         quantize_pass(0, HALF, S)
-        place(0, 0, CHUNK, grouped[HALF][:, HALF * PACK : HALF * PACK + 2 * CHUNK].bitcast(F32))
-        place(1, 0, HALF, y_sb[1][:, 0:HALF])
+        quantize_chunk()
+        place(0, 0, CHUNK, grouped[HALF][1][:, 0 : 2 * CHUNK].bitcast(F32))
+        for b in range(1, EARLY):
+            place(b, 0, CHUNK, y_sb[b][:, 0:CHUNK])
         interleave(1, HALF, S)
         quantize_pass(1, HALF, S)
-        place(2, 0, HALF, y_sb[2][:, 0:HALF])
-        place(3, 0, S, y_sb[3][:])
-        place(0, CHUNK, S, y_sb[0][:, CHUNK:S])
-        place(1, HALF, S, y_sb[1][:, HALF:S])
-        place(2, HALF, S, y_sb[2][:, HALF:S])
+        for b in range(EARLY):
+            place(b, CHUNK, HALF, picked1[:, b * S + HALF : b * S + HALF + CHUNK])
+        for b in range(EARLY):
+            place(b, HALF, S, y_sb[b][:, HALF:S])
         for b in range(4, BLOCKS):
             place(b, 0, S, y_sb[b][:])

@@ -22,6 +22,8 @@ CHUNK = 128
 EARLY = 4
 PIECES = ((0, CHUNK), (CHUNK, HALF), (HALF, S))
 WINDOWS = 4
+SQUARE = 32
+GROUP = 16
 
 
 def tile_list_hboth_none_kernel(tc, xT, w_words, w_scales, wgt, wgo, offs, offs2, out):
@@ -36,7 +38,10 @@ def tile_list_hboth_none_kernel(tc, xT, w_words, w_scales, wgt, wgo, offs, offs2
         plane = [[held.tile([P, T], F32, name=f"plane{a}_{t}", align_bytes=64) for t in range(PACK)] for a in range(PASSES)]
         picked0 = held.tile([P, PACK, S], F32, name="picked0")
         picked1 = held.tile([P, PACK * S], F32, name="picked1", align_bytes=64)
-        wgt_sb = held.tile([P, S], F32, name="wgt_sb")
+        wgt_rows = held.tile([P, SQUARE], F32, name="wgt_rows", align_bytes=64)
+        wgt_turned = held.tile([P, SQUARE], F32, name="wgt_turned", align_bytes=64)
+        wgt_repeated = held.tile([P, S], F32, name="wgt_repeated", align_bytes=64)
+        wgt_sb = held.tile([P, S], F32, name="wgt_sb", align_bytes=64)
         grouped_first = [held.tile([P, CHUNK * PACK], BF16, name=f"grouped_first{a}", align_bytes=64) for a in range(PASSES)]
         grouped_chunk = held.tile([P, PASSES * CHUNK * PACK], BF16, name="grouped_chunk", align_bytes=64)
         grouped_half = held.tile([P, PASSES * HALF * PACK], BF16, name="grouped_half", align_bytes=64)
@@ -51,22 +56,18 @@ def tile_list_hboth_none_kernel(tc, xT, w_words, w_scales, wgt, wgo, offs, offs2
             codes[lo] = [both[:, a * (hi - lo) : (a + 1) * (hi - lo)] for a in range(PASSES)]
             xsc[lo] = held.tile([P, PASSES * (hi - lo)], U8, name=f"xsc{lo}", align_bytes=64)
             codes[lo].append(both[:])
-        zeroed = [held.tile([P, T], F32, name=f"window{i}") for i in range(WINDOWS)]
-        window = [zeroed[b % WINDOWS] for b in range(BLOCKS)]
+        window = []
         y_sb = [held.tile([P, S], F32, name=f"y{b}") for b in range(BLOCKS)]
         bank = [psum.tile([P, S], F32, name=f"bank{b}") for b in range(BLOCKS)]
 
         nc.vector.memset(wsc[:].bitcast(I32), 0)
-        for tile in zeroed:
-            nc.vector.memset(tile[:], 0.0)
 
         rows = xT.rearrange("(a p t) n -> a t p n", p=P, t=PACK)
         words = w_words.bitcast(I32).rearrange("a p n -> p a n")
         scale_rows = w_scales.bitcast(I32).rearrange("a (q r) n -> r q a n", r=4)
+        nc.sync.dma_start(wgt_rows[:], wgt.rearrange("(g r) (b c) -> g r b c", r=GROUP, c=SQUARE)[:, 0])
         nc.sync.dma_start(plane[0][0][:], rows[0, 0])
-        nc.scalar.dma_start(wgt_sb[:, 0:CHUNK], wgt[:, 0:CHUNK])
         nc.sync.dma_start(list_in[:], offs)
-        nc.sync.dma_start(wgt_sb[:, CHUNK:S], wgt[:, CHUNK:S])
         for a in range(PASSES):
             for t in range(PACK):
                 if a + t > 0:
@@ -78,6 +79,22 @@ def tile_list_hboth_none_kernel(tc, xT, w_words, w_scales, wgt, wgo, offs, offs2
         nc.sync.dma_start(list_out[:], offs2)
         nc.sync.dma_start(wgo_sb[:], wgo)
         nc.sync.dma_start(w_late[:].bitcast(I32), words[:, :, split : M // 2])
+
+        nc.vector.transpose(wgt_turned[:], wgt_rows[:])
+        turned = wgt_turned[:].rearrange("p (h b) -> p b h", h=2)
+        for lo in (0, HALF):
+            b0, b1 = lo // SQUARE, (lo + HALF) // SQUARE
+            nc.vector.tensor_copy(
+                wgt_repeated[:, lo : lo + HALF].rearrange("p (b h r) -> p b h r", h=2, r=GROUP),
+                turned[:, b0:b1].unsqueeze(3).to_broadcast([P, b1 - b0, 2, GROUP]),
+            )
+        for lo in (0, HALF):
+            nc.vector.transpose(wgt_sb[:, lo : lo + HALF], wgt_repeated[:, lo : lo + HALF])
+
+        def zero_window(t):
+            tile = held.tile([P, T], F32, name=f"window{t}", tag=f"plane0_{t}", align_bytes=64)
+            nc.gpsimd.memset(tile[:], 0.0)
+            window.append(tile)
 
         def picked(a, lo, hi):
             if a == 0:
@@ -132,24 +149,26 @@ def tile_list_hboth_none_kernel(tc, xT, w_words, w_scales, wgt, wgo, offs, offs2
                 multiply(b, c, acc[:, c : c + CHUNK])
             nc.scalar.copy(y, acc[:, lo:hi])
             nc.vector.tensor_tensor(
-                window[b][:].indirect(list_out[:, lo // 16 : hi // 16]),
+                window[b % WINDOWS][:].indirect(list_out[:, lo // 16 : hi // 16]),
                 y,
                 wgo_sb[:, lo:hi],
                 MULT,
             )
-            if hi == S and EARLY <= b < BLOCKS - 1:
-                nc.sync.dma_start(out[P * b : P * (b + 1), :], window[b][:])
-            elif hi == S and b < EARLY:
-                nc.sync.dma_start(out[P * b : P * (b + 1), 0 : T // 2], window[b][:, 0 : T // 2])
-                nc.sync.dma_start(out[P * b : P * (b + 1), T // 2 : T], window[b][:, T // 2 : T])
+            if hi == S and EARLY < b < BLOCKS - 1:
+                nc.sync.dma_start(out[P * b : P * (b + 1), :], window[b % WINDOWS][:])
+            elif hi == S and b <= EARLY:
+                nc.sync.dma_start(out[P * b : P * (b + 1), 0 : T // 2], window[b % WINDOWS][:, 0 : T // 2])
+                nc.sync.dma_start(out[P * b : P * (b + 1), T // 2 : T], window[b % WINDOWS][:, T // 2 : T])
             elif hi == S:
-                nc.sync.dma_start(out[P * b : P * (b + 1), 0 : T // 2], window[b][:, 0 : T // 2])
-                nc.scalar.dma_start(out[P * b : P * (b + 1), T // 2 : T], window[b][:, T // 2 : T])
+                nc.sync.dma_start(out[P * b : P * (b + 1), 0 : T // 2], window[b % WINDOWS][:, 0 : T // 2])
+                nc.scalar.dma_start(out[P * b : P * (b + 1), T // 2 : T], window[b % WINDOWS][:, T // 2 : T])
 
-        gather(0, 0, 0, CHUNK)
-        gather(0, 0, CHUNK, S)
+        gather(0, 0, 0, HALF)
+        gather(0, 0, HALF, S)
+        zero_window(0)
         for t in range(1, PACK):
             gather(0, t, 0, S)
+            zero_window(t)
         for lo, hi in PIECES:
             interleave(0, lo, hi)
         gather(1, 0, 0, S)

@@ -19,16 +19,20 @@ PASSES = K // (P * PACK)
 BLOCKS = M // P
 HALF = S // 2
 CHUNK = 128
+CHUNKS = S // CHUNK
 EARLY = 4
-PIECES = ((0, CHUNK), (CHUNK, HALF), (HALF, S))
-WINDOWS = 4
 SQUARE = 32
 GROUP = 16
+REGION = 2048
 
 
 def tile_list_hboth_none_kernel(tc, xT, w_words, w_scales, wgt, wgo, offs, offs2, out):
     nc = tc.nc
-    with tc.tile_pool(name="held", bufs=1) as held, tc.psum_pool(name="psum", bufs=1) as psum:
+    with (
+        tc.tile_pool(name="held", bufs=1) as held,
+        tc.tile_pool(name="shared", bufs=1) as shared,
+        tc.psum_pool(name="psum", bufs=1) as psum,
+    ):
         list_in = held.tile([P, S // 16], U16, name="list_in")
         list_out = held.tile([P, S // 16], U16, name="list_out")
         wgo_sb = held.tile([P, S], F32, name="wgo_sb")
@@ -42,25 +46,20 @@ def tile_list_hboth_none_kernel(tc, xT, w_words, w_scales, wgt, wgo, offs, offs2
         wgt_turned = held.tile([P, SQUARE], F32, name="wgt_turned", align_bytes=64)
         wgt_repeated = held.tile([P, S], F32, name="wgt_repeated", align_bytes=64)
         wgt_sb = held.tile([P, S], F32, name="wgt_sb", align_bytes=64)
-        grouped_first = [held.tile([P, CHUNK * PACK], BF16, name=f"grouped_first{a}", align_bytes=64) for a in range(PASSES)]
-        grouped_chunk = held.tile([P, PASSES * CHUNK * PACK], BF16, name="grouped_chunk", align_bytes=64)
-        grouped_half = held.tile([P, PASSES * HALF * PACK], BF16, name="grouped_half", align_bytes=64)
-        grouped = {
-            0: [tile[:] for tile in grouped_first],
-            CHUNK: [grouped_chunk[:, a * CHUNK * PACK : (a + 1) * CHUNK * PACK] for a in range(PASSES)],
-            HALF: [grouped_half[:, a * HALF * PACK : (a + 1) * HALF * PACK] for a in range(PASSES)],
-        }
-        codes, xsc = {}, {}
-        for lo, hi in PIECES:
-            both = held.tile([P, PASSES * (hi - lo)], U32, name=f"codes{lo}", align_bytes=64)
-            codes[lo] = [both[:, a * (hi - lo) : (a + 1) * (hi - lo)] for a in range(PASSES)]
-            xsc[lo] = held.tile([P, PASSES * (hi - lo)], U8, name=f"xsc{lo}", align_bytes=64)
-            codes[lo].append(both[:])
-        window = []
-        y_sb = [held.tile([P, S], F32, name=f"y{b}") for b in range(BLOCKS)]
+        grouped0 = held.tile([P, 3 * CHUNK * PACK], BF16, name="grouped0", align_bytes=64)
+        grouped1_first = held.tile([P, CHUNK * PACK], BF16, name="grouped1_first", align_bytes=64)
+        codes_first = [held.tile([P, CHUNK], U32, name=f"codes_first{a}", align_bytes=64) for a in range(PASSES)]
+        xsc = [held.tile([P, S], U8, name=f"xsc{a}", align_bytes=64) for a in range(PASSES)]
+        y_first = [
+            shared.tile([P, CHUNK], F32, name=f"y_first{b}", align_bytes=64, offset=b * REGION + 768) for b in range(BLOCKS)
+        ]
+        y_rest = [held.tile([P, S - CHUNK], F32, name=f"y_rest{b}") for b in range(BLOCKS)]
         bank = [psum.tile([P, S], F32, name=f"bank{b}") for b in range(BLOCKS)]
+        window = [held.tile([P, T], F32, name="window0", align_bytes=64)]
+        codes = {(a, 0): codes_first[a][:] for a in range(PASSES)}
 
         nc.vector.memset(wsc[:].bitcast(I32), 0)
+        nc.vector.memset(window[0][:], 0.0)
 
         rows = xT.rearrange("(a p t) n -> a t p n", p=P, t=PACK)
         words = w_words.bitcast(I32).rearrange("a p n -> p a n")
@@ -80,6 +79,11 @@ def tile_list_hboth_none_kernel(tc, xT, w_words, w_scales, wgt, wgo, offs, offs2
         nc.sync.dma_start(wgo_sb[:], wgo)
         nc.sync.dma_start(w_late[:].bitcast(I32), words[:, :, split : M // 2])
 
+        def zero_window(tag):
+            tile = held.tile([P, T], F32, name=f"window{len(window)}", tag=tag, align_bytes=64)
+            nc.gpsimd.memset(tile[:], 0.0)
+            window.append(tile)
+
         nc.vector.transpose(wgt_turned[:], wgt_rows[:])
         turned = wgt_turned[:].rearrange("p (h b) -> p b h", h=2)
         for lo in (0, HALF):
@@ -88,13 +92,10 @@ def tile_list_hboth_none_kernel(tc, xT, w_words, w_scales, wgt, wgo, offs, offs2
                 wgt_repeated[:, lo : lo + HALF].rearrange("p (b h r) -> p b h r", h=2, r=GROUP),
                 turned[:, b0:b1].unsqueeze(3).to_broadcast([P, b1 - b0, 2, GROUP]),
             )
+        zero_window("wgt_turned")
         for lo in (0, HALF):
             nc.vector.transpose(wgt_sb[:, lo : lo + HALF], wgt_repeated[:, lo : lo + HALF])
-
-        def zero_window(t):
-            tile = held.tile([P, T], F32, name=f"window{t}", tag=f"plane0_{t}", align_bytes=64)
-            nc.gpsimd.memset(tile[:], 0.0)
-            window.append(tile)
+        zero_window("wgt_repeated")
 
         def picked(a, lo, hi):
             if a == 0:
@@ -111,93 +112,88 @@ def tile_list_hboth_none_kernel(tc, xT, w_words, w_scales, wgt, wgo, offs, offs2
                 MULT,
             )
 
-        def interleave(a, lo, hi, pairs=slice(0, 2)):
-            dst = grouped[lo][a].rearrange("p (c i u v) -> p c u v i", i=4, u=2, v=2)
+        def interleave(grouped, a, lo, hi, pairs=slice(0, 2)):
+            dst = grouped.rearrange("p (c i u v) -> p c u v i", i=4, u=2, v=2)
             src = picked(a, lo, hi).rearrange("p u v (c i) -> p c u v i", i=4)
             nc.scalar.copy(dst[:, :, pairs], src[:, :, pairs])
 
-        def quantize_chunk():
-            nc.vector.quantize_mx(out=codes[CHUNK][PASSES].bitcast(FP8X4), scales=xsc[CHUNK][:], in_=grouped_chunk[:])
+        def quantize(a, lo, hi, grouped, into):
+            nc.vector.quantize_mx(out=into.bitcast(FP8X4), scales=xsc[a][:, lo:hi], in_=grouped)
+            for c in range(lo, hi, CHUNK):
+                codes[a, c] = into[:, c - lo : c - lo + CHUNK]
 
-        def quantize_pass(a, lo, hi):
-            width = hi - lo
-            nc.vector.quantize_mx(
-                out=codes[lo][a].bitcast(FP8X4),
-                scales=xsc[lo][:, a * width : (a + 1) * width],
-                in_=grouped[lo][a],
-            )
-
-        def multiply(b, c, into):
+        def multiply(b, c):
             w_sb, first = (w_early, b) if b < EARLY else (w_late, b - EARLY)
-            lo, hi = [piece for piece in PIECES if piece[0] <= c < piece[1]][0]
-            order = range(PASSES) if b < 2 else range(PASSES - 1, -1, -1)
+            order = range(PASSES) if b < 2 and c == 0 else range(PASSES - 1, -1, -1)
             for a in order:
-                at = a * (hi - lo) + c - lo
                 nc.tensor.matmul_mx(
-                    out=into,
+                    out=bank[b][:, c : c + CHUNK],
                     lhsT=w_sb[:, a, 2 * P * first : 2 * P * (first + 1)].bitcast(FP4X4),
                     lhsT_scale=wsc[:, a, P * b : P * (b + 1)],
-                    rhs=codes[lo][a][:, c - lo : c - lo + CHUNK].bitcast(FP8X4),
-                    rhs_scale=xsc[lo][:, at : at + CHUNK],
+                    rhs=codes[a, c].bitcast(FP8X4),
+                    rhs_scale=xsc[a][:, c : c + CHUNK],
                     start=(a == order[0]),
                     stop=(a == order[-1]),
                 )
 
-        def place(b, lo, hi, y, acc=None):
-            acc = bank[b] if acc is None else acc
-            for c in range(lo, hi, CHUNK):
-                multiply(b, c, acc[:, c : c + CHUNK])
-            nc.scalar.copy(y, acc[:, lo:hi])
-            nc.vector.tensor_tensor(
-                window[b % WINDOWS][:].indirect(list_out[:, lo // 16 : hi // 16]),
-                y,
-                wgo_sb[:, lo:hi],
-                MULT,
-            )
-            if hi == S and EARLY < b < BLOCKS - 1:
-                nc.sync.dma_start(out[P * b : P * (b + 1), :], window[b % WINDOWS][:])
-            elif hi == S and b <= EARLY:
-                nc.sync.dma_start(out[P * b : P * (b + 1), 0 : T // 2], window[b % WINDOWS][:, 0 : T // 2])
-                nc.sync.dma_start(out[P * b : P * (b + 1), T // 2 : T], window[b % WINDOWS][:, T // 2 : T])
-            elif hi == S:
-                nc.sync.dma_start(out[P * b : P * (b + 1), 0 : T // 2], window[b % WINDOWS][:, 0 : T // 2])
-                nc.scalar.dma_start(out[P * b : P * (b + 1), T // 2 : T], window[b % WINDOWS][:, T // 2 : T])
+        def place(b, lo, hi, y):
+            chunks = range(lo, hi, CHUNK)
+            for c in chunks if b < 2 else reversed(chunks):
+                multiply(b, c)
+            nc.scalar.copy(y, bank[b][:, lo:hi])
+            nc.vector.tensor_tensor(window[b][:].indirect(list_out[:, lo // 16 : hi // 16]), y, wgo_sb[:, lo:hi], MULT)
+
+        def store(b):
+            rows_out = out[P * b : P * (b + 1)]
+            if b in (5, 6):
+                nc.sync.dma_start(rows_out, window[b][:])
+            else:
+                nc.sync.dma_start(rows_out[:, 0 : T // 2], window[b][:, 0 : T // 2])
+                nc.sync.dma_start(rows_out[:, T // 2 : T], window[b][:, T // 2 : T])
+
+        def late_codes(b, width):
+            return shared.tile([P, width], U32, name=f"codes_behind{b}", align_bytes=64, offset=b * REGION + 1024)[:]
+
+        def late_pass0(b, lo, hi):
+            quantize(0, lo, hi, grouped0[:, lo * PACK : hi * PACK], late_codes(b, hi - lo))
+
+        def late_piece(b, a, lo):
+            grouped = shared.tile([P, CHUNK * PACK], BF16, name=f"grouped_behind{b}", align_bytes=64, offset=b * REGION)
+            interleave(grouped[:], a, lo, lo + CHUNK)
+            quantize(a, lo, lo + CHUNK, grouped[:], late_codes(b + 1, CHUNK))
 
         gather(0, 0, 0, HALF)
         gather(0, 0, HALF, S)
-        zero_window(0)
+        zero_window("plane0_0")
         for t in range(1, PACK):
             gather(0, t, 0, S)
-            zero_window(t)
-        for lo, hi in PIECES:
-            interleave(0, lo, hi)
+            if t < PACK - 1:
+                zero_window(f"plane0_{t}")
+        interleave(grouped0[:, 0 : CHUNK * PACK], 0, 0, CHUNK)
+        interleave(grouped0[:, CHUNK * PACK : 3 * CHUNK * PACK], 0, CHUNK, 3 * CHUNK)
         gather(1, 0, 0, S)
-        quantize_pass(0, 0, CHUNK)
+        quantize(0, 0, CHUNK, grouped0[:, 0 : CHUNK * PACK], codes_first[0][:])
+        zero_window("plane1_0")
         gather(1, 1, 0, S)
-        interleave(1, 0, CHUNK, slice(0, 1))
-        interleave(1, CHUNK, HALF, slice(0, 1))
-        gather(1, 2, 0, HALF)
+        zero_window("plane1_1")
+        interleave(grouped1_first[:], 1, 0, CHUNK, slice(0, 1))
+        gather(1, 2, 0, CHUNK)
         gather(1, 3, 0, CHUNK, last_pair[:, 1, :])
         gather(1, 3, CHUNK, S)
         nc.scalar.copy(
-            grouped[0][1].rearrange("p (c i u v) -> p c u v i", i=4, u=2, v=2)[:, :, 1],
+            grouped1_first[:].rearrange("p (c i u v) -> p c u v i", i=4, u=2, v=2)[:, :, 1],
             last_pair.rearrange("p v (c i) -> p c v i", i=4),
         )
-        interleave(1, CHUNK, HALF, slice(1, 2))
-        quantize_pass(1, 0, CHUNK)
-        gather(1, 2, HALF, S)
-        late = held.tile([P, HALF], U32, name="codes_late", tag="grouped_first1", align_bytes=64)
-        codes[HALF][0] = late[:]
-        quantize_pass(0, HALF, S)
-        quantize_chunk()
-        place(0, 0, CHUNK, grouped[HALF][1][:, 0 : 2 * CHUNK].bitcast(F32))
-        for b in range(1, EARLY):
-            place(b, 0, CHUNK, y_sb[b][:, 0:CHUNK])
-        interleave(1, HALF, S)
-        quantize_pass(1, HALF, S)
-        for b in range(EARLY):
-            place(b, CHUNK, HALF, picked1[:, b * S + HALF : b * S + HALF + CHUNK])
-        for b in range(EARLY):
-            place(b, HALF, S, y_sb[b][:, HALF:S])
-        for b in range(4, BLOCKS):
-            place(b, 0, S, y_sb[b][:])
+        quantize(1, 0, CHUNK, grouped1_first[:], codes_first[1][:])
+        gather(1, 2, CHUNK, S)
+        for b in range(BLOCKS):
+            place(b, 0, CHUNK, y_first[b][:])
+            if b == 1:
+                late_pass0(0, CHUNK, 3 * CHUNK)
+            if 2 <= b < 5:
+                late_piece(b - 2, 1, (b - 1) * CHUNK)
+            if b == 5:
+                late_piece(b - 2, 0, 3 * CHUNK)
+        for b in range(BLOCKS):
+            place(b, CHUNK, S, y_rest[b][:])
+            store(b)

@@ -21,18 +21,13 @@ HALF = S // 2
 CHUNK = 128
 CHUNKS = S // CHUNK
 EARLY = 4
-SQUARE = 32
-GROUP = 16
-REGION = 2048
+WINDOWS = 4
+SLIVER = 64
 
 
 def tile_list_hboth_none_kernel(tc, xT, w_words, w_scales, wgt, wgo, offs, offs2, out):
     nc = tc.nc
-    with (
-        tc.tile_pool(name="held", bufs=1) as held,
-        tc.tile_pool(name="shared", bufs=1) as shared,
-        tc.psum_pool(name="psum", bufs=1) as psum,
-    ):
+    with tc.tile_pool(name="held", bufs=1) as held, tc.psum_pool(name="psum", bufs=1) as psum:
         list_in = held.tile([P, S // 16], U16, name="list_in")
         list_out = held.tile([P, S // 16], U16, name="list_out")
         wgo_sb = held.tile([P, S], F32, name="wgo_sb")
@@ -40,33 +35,31 @@ def tile_list_hboth_none_kernel(tc, xT, w_words, w_scales, wgt, wgo, offs, offs2
         w_late = held.tile([P, PASSES, 2 * P * (BLOCKS - EARLY)], U8, name="w_late", align_bytes=64)
         wsc = held.tile([P, PASSES, M], U8, name="wsc", align_bytes=64)
         plane = [[held.tile([P, T], F32, name=f"plane{a}_{t}", align_bytes=64) for t in range(PACK)] for a in range(PASSES)]
-        picked0 = held.tile([P, PACK, S], F32, name="picked0")
-        picked1 = held.tile([P, PACK * S], F32, name="picked1", align_bytes=64)
-        wgt_rows = held.tile([P, SQUARE], F32, name="wgt_rows", align_bytes=64)
-        wgt_turned = held.tile([P, SQUARE], F32, name="wgt_turned", align_bytes=64)
-        wgt_repeated = held.tile([P, S], F32, name="wgt_repeated", align_bytes=64)
+        picks = [held.tile([P, PACK * S], F32, name=f"picks{a}", align_bytes=64) for a in range(PASSES)]
         wgt_sb = held.tile([P, S], F32, name="wgt_sb", align_bytes=64)
-        grouped0 = held.tile([P, 3 * CHUNK * PACK], BF16, name="grouped0", align_bytes=64)
-        grouped1_first = held.tile([P, CHUNK * PACK], BF16, name="grouped1_first", align_bytes=64)
-        codes_first = [held.tile([P, CHUNK], U32, name=f"codes_first{a}", align_bytes=64) for a in range(PASSES)]
-        xsc = [held.tile([P, S], U8, name=f"xsc{a}", align_bytes=64) for a in range(PASSES)]
-        y_first = [
-            shared.tile([P, CHUNK], F32, name=f"y_first{b}", align_bytes=64, offset=b * REGION + 768) for b in range(BLOCKS)
-        ]
-        y_rest = [held.tile([P, S - CHUNK], F32, name=f"y_rest{b}") for b in range(BLOCKS)]
+        grouped_first = [held.tile([P, CHUNK * PACK], BF16, name=f"grouped_first{a}", align_bytes=64) for a in range(PASSES)]
+        grouped_second = held.tile([P, PASSES * CHUNK * PACK], BF16, name="grouped_second", align_bytes=64)
+        grouped_half = held.tile([P, HALF * PACK], BF16, name="grouped_half", align_bytes=64)
+        grouped_late = held.tile([P, SLIVER * PACK], BF16, name="grouped_late", align_bytes=64)
+        codes_front = held.tile([P, PASSES * HALF], U32, name="codes_front", align_bytes=64)
+        codes_late = held.tile([P, HALF], U32, name="codes_late", align_bytes=64)
+        xsc = held.tile([P, PASSES * S], U8, name="xsc", align_bytes=64)
+        codes_half = {1: codes_late}
+        y_sb = [held.tile([P, S], F32, name=f"y{b}") for b in range(BLOCKS)]
         bank = [psum.tile([P, S], F32, name=f"bank{b}") for b in range(BLOCKS)]
-        window = [held.tile([P, T], F32, name="window0", align_bytes=64)]
-        codes = {(a, 0): codes_first[a][:] for a in range(PASSES)}
+        window = [held.tile([P, T], F32, name=f"window{i}", align_bytes=64) for i in range(WINDOWS)]
 
         nc.vector.memset(wsc[:].bitcast(I32), 0)
-        nc.vector.memset(window[0][:], 0.0)
+        for tile in window:
+            nc.vector.memset(tile[:], 0.0)
 
         rows = xT.rearrange("(a p t) n -> a t p n", p=P, t=PACK)
         words = w_words.bitcast(I32).rearrange("a p n -> p a n")
         scale_rows = w_scales.bitcast(I32).rearrange("a (q r) n -> r q a n", r=4)
-        nc.sync.dma_start(wgt_rows[:], wgt.rearrange("(g r) (b c) -> g r b c", r=GROUP, c=SQUARE)[:, 0])
         nc.sync.dma_start(plane[0][0][:], rows[0, 0])
+        nc.scalar.dma_start(wgt_sb[:, 0:CHUNK], wgt[:, 0:CHUNK])
         nc.sync.dma_start(list_in[:], offs)
+        nc.sync.dma_start(wgt_sb[:, CHUNK:S], wgt[:, CHUNK:S])
         for a in range(PASSES):
             for t in range(PACK):
                 if a + t > 0:
@@ -79,30 +72,13 @@ def tile_list_hboth_none_kernel(tc, xT, w_words, w_scales, wgt, wgo, offs, offs2
         nc.sync.dma_start(wgo_sb[:], wgo)
         nc.sync.dma_start(w_late[:].bitcast(I32), words[:, :, split : M // 2])
 
-        def zero_window(tag):
-            tile = held.tile([P, T], F32, name=f"window{len(window)}", tag=tag, align_bytes=64)
-            nc.gpsimd.memset(tile[:], 0.0)
-            window.append(tile)
-
-        nc.vector.transpose(wgt_turned[:], wgt_rows[:])
-        turned = wgt_turned[:].rearrange("p (h b) -> p b h", h=2)
-        for lo in (0, HALF):
-            b0, b1 = lo // SQUARE, (lo + HALF) // SQUARE
-            nc.vector.tensor_copy(
-                wgt_repeated[:, lo : lo + HALF].rearrange("p (b h r) -> p b h r", h=2, r=GROUP),
-                turned[:, b0:b1].unsqueeze(3).to_broadcast([P, b1 - b0, 2, GROUP]),
-            )
-        zero_window("wgt_turned")
-        for lo in (0, HALF):
-            nc.vector.transpose(wgt_sb[:, lo : lo + HALF], wgt_repeated[:, lo : lo + HALF])
-        zero_window("wgt_repeated")
-
         def picked(a, lo, hi):
-            if a == 0:
-                return picked0[:, :, lo:hi].rearrange("p (u v) c -> p u v c", u=2)
-            return picked1[:].rearrange("p (u v c) -> p u v c", u=2, v=2)[:, :, :, lo:hi]
+            return picks[a][:].rearrange("p (u v c) -> p u v c", u=2, v=2)[:, :, :, lo:hi]
 
-        last_pair = picked1[:, 2 * S : 3 * S].rearrange("p (v c) -> p v c", v=2)[:, :, 0:CHUNK]
+        def left(a, t, lo, hi):
+            return picks[a][:, t * S + lo : t * S + hi]
+
+        last_pair = picks[1][:, 2 * S : 3 * S].rearrange("p (v c) -> p v c", v=2)[:, :, 0:CHUNK]
 
         def gather(a, t, lo, hi, dst=None):
             nc.vector.tensor_tensor(
@@ -117,21 +93,28 @@ def tile_list_hboth_none_kernel(tc, xT, w_words, w_scales, wgt, wgo, offs, offs2
             src = picked(a, lo, hi).rearrange("p u v (c i) -> p c u v i", i=4)
             nc.scalar.copy(dst[:, :, pairs], src[:, :, pairs])
 
-        def quantize(a, lo, hi, grouped, into):
-            nc.vector.quantize_mx(out=into.bitcast(FP8X4), scales=xsc[a][:, lo:hi], in_=grouped)
-            for c in range(lo, hi, CHUNK):
-                codes[a, c] = into[:, c - lo : c - lo + CHUNK]
+        def operand(a, lo, width):
+            if lo < HALF:
+                at = PASSES * lo + a * CHUNK
+                return codes_front[:, at : at + width].bitcast(FP8X4), xsc[:, at : at + width]
+            at = (PASSES + a - 1) * HALF + lo
+            return codes_half[a][:, lo - HALF : lo - HALF + width].bitcast(FP8X4), xsc[:, at : at + width]
+
+        def quantize(a, lo, width, grouped):
+            codes, scales = operand(a, lo, width)
+            nc.vector.quantize_mx(out=codes, scales=scales, in_=grouped)
 
         def multiply(b, c):
             w_sb, first = (w_early, b) if b < EARLY else (w_late, b - EARLY)
-            order = range(PASSES) if b < 2 and c == 0 else range(PASSES - 1, -1, -1)
+            order = range(PASSES) if b < 2 else range(PASSES - 1, -1, -1)
             for a in order:
+                codes, scales = operand(a, c, CHUNK)
                 nc.tensor.matmul_mx(
                     out=bank[b][:, c : c + CHUNK],
                     lhsT=w_sb[:, a, 2 * P * first : 2 * P * (first + 1)].bitcast(FP4X4),
                     lhsT_scale=wsc[:, a, P * b : P * (b + 1)],
-                    rhs=codes[a, c].bitcast(FP8X4),
-                    rhs_scale=xsc[a][:, c : c + CHUNK],
+                    rhs=codes,
+                    rhs_scale=scales,
                     start=(a == order[0]),
                     stop=(a == order[-1]),
                 )
@@ -141,59 +124,63 @@ def tile_list_hboth_none_kernel(tc, xT, w_words, w_scales, wgt, wgo, offs, offs2
             for c in chunks if b < 2 else reversed(chunks):
                 multiply(b, c)
             nc.scalar.copy(y, bank[b][:, lo:hi])
-            nc.vector.tensor_tensor(window[b][:].indirect(list_out[:, lo // 16 : hi // 16]), y, wgo_sb[:, lo:hi], MULT)
+            nc.vector.tensor_tensor(window[b % WINDOWS][:].indirect(list_out[:, lo // 16 : hi // 16]), y, wgo_sb[:, lo:hi], MULT)
 
         def store(b):
-            rows_out = out[P * b : P * (b + 1)]
-            if b in (5, 6):
-                nc.sync.dma_start(rows_out, window[b][:])
+            rows_out, source = out[P * b : P * (b + 1)], window[b % WINDOWS]
+            if EARLY <= b < BLOCKS - 1:
+                nc.sync.dma_start(rows_out, source[:])
             else:
-                nc.sync.dma_start(rows_out[:, 0 : T // 2], window[b][:, 0 : T // 2])
-                nc.sync.dma_start(rows_out[:, T // 2 : T], window[b][:, T // 2 : T])
+                second = nc.scalar if b == BLOCKS - 1 else nc.sync
+                nc.sync.dma_start(rows_out[:, 0 : T // 2], source[:, 0 : T // 2])
+                second.dma_start(rows_out[:, T // 2 : T], source[:, T // 2 : T])
 
-        def late_codes(b, width):
-            return shared.tile([P, width], U32, name=f"codes_behind{b}", align_bytes=64, offset=b * REGION + 1024)[:]
-
-        def late_pass0(b, lo, hi):
-            quantize(0, lo, hi, grouped0[:, lo * PACK : hi * PACK], late_codes(b, hi - lo))
-
-        def late_piece(b, a, lo):
-            grouped = shared.tile([P, CHUNK * PACK], BF16, name=f"grouped_behind{b}", align_bytes=64, offset=b * REGION)
-            interleave(grouped[:], a, lo, lo + CHUNK)
-            quantize(a, lo, lo + CHUNK, grouped[:], late_codes(b + 1, CHUNK))
-
-        gather(0, 0, 0, HALF)
-        gather(0, 0, HALF, S)
-        zero_window("plane0_0")
+        second = [grouped_second[:, a * CHUNK * PACK : (a + 1) * CHUNK * PACK] for a in range(PASSES)]
+        gather(0, 0, 0, CHUNK)
+        gather(0, 0, CHUNK, S)
         for t in range(1, PACK):
             gather(0, t, 0, S)
-            if t < PACK - 1:
-                zero_window(f"plane0_{t}")
-        interleave(grouped0[:, 0 : CHUNK * PACK], 0, 0, CHUNK)
-        interleave(grouped0[:, CHUNK * PACK : 3 * CHUNK * PACK], 0, CHUNK, 3 * CHUNK)
+        interleave(grouped_first[0][:], 0, 0, CHUNK)
+        interleave(second[0], 0, CHUNK, HALF)
+        interleave(grouped_half[:], 0, HALF, S)
         gather(1, 0, 0, S)
-        quantize(0, 0, CHUNK, grouped0[:, 0 : CHUNK * PACK], codes_first[0][:])
-        zero_window("plane1_0")
+        quantize(0, 0, CHUNK, grouped_first[0][:])
         gather(1, 1, 0, S)
-        zero_window("plane1_1")
-        interleave(grouped1_first[:], 1, 0, CHUNK, slice(0, 1))
-        gather(1, 2, 0, CHUNK)
+        interleave(grouped_first[1][:], 1, 0, CHUNK, slice(0, 1))
+        interleave(second[1], 1, CHUNK, HALF, slice(0, 1))
+        gather(1, 2, 0, HALF)
         gather(1, 3, 0, CHUNK, last_pair[:, 1, :])
         gather(1, 3, CHUNK, S)
         nc.scalar.copy(
-            grouped1_first[:].rearrange("p (c i u v) -> p c u v i", i=4, u=2, v=2)[:, :, 1],
+            grouped_first[1][:].rearrange("p (c i u v) -> p c u v i", i=4, u=2, v=2)[:, :, 1],
             last_pair.rearrange("p v (c i) -> p c v i", i=4),
         )
-        quantize(1, 0, CHUNK, grouped1_first[:], codes_first[1][:])
-        gather(1, 2, CHUNK, S)
-        for b in range(BLOCKS):
-            place(b, 0, CHUNK, y_first[b][:])
-            if b == 1:
-                late_pass0(0, CHUNK, 3 * CHUNK)
-            if 2 <= b < 5:
-                late_piece(b - 2, 1, (b - 1) * CHUNK)
-            if b == 5:
-                late_piece(b - 2, 0, 3 * CHUNK)
-        for b in range(BLOCKS):
-            place(b, CHUNK, S, y_rest[b][:])
+        interleave(second[1], 1, CHUNK, HALF, slice(1, 2))
+        quantize(1, 0, CHUNK, grouped_first[1][:])
+        gather(1, 2, HALF, S)
+        codes_half[0] = held.tile([P, HALF], U32, name="codes_half", tag="grouped_first1", align_bytes=64)
+        quantize(0, HALF, HALF, grouped_half[:])
+        quantize(0, CHUNK, PASSES * CHUNK, grouped_second[:])
+
+        slivers = range(HALF, S, SLIVER)
+        steps = [(b, lo) for lo in (0, CHUNK) for b in range(EARLY)]
+        staged = [y_sb[b][:, lo : lo + CHUNK] for b, lo in steps]
+        staged[0] = grouped_late[:].bitcast(F32)
+        grouped = [grouped_late[:]]
+        for i, lo in enumerate(slivers):
+            staged[i + 3] = left(1, i, lo - SLIVER, lo + SLIVER)
+            if i > 0:
+                grouped.append(left(1, (i + 1) % PACK, lo - 2 * SLIVER, lo).bitcast(BF16))
+        staged[-1] = left(1, 1, S - CHUNK, S)
+        for i, (b, lo) in enumerate(steps):
+            place(b, lo, lo + CHUNK, staged[i])
+            if 2 <= i < 2 + len(slivers):
+                at = slivers[i - 2]
+                interleave(grouped[i - 2], 1, at, at + SLIVER)
+                quantize(1, at, SLIVER, grouped[i - 2])
+        for b in range(EARLY):
+            place(b, HALF, S, y_sb[b][:, HALF:S])
+            store(b)
+        for b in range(EARLY, BLOCKS):
+            place(b, 0, S, y_sb[b][:])
             store(b)

@@ -23,11 +23,16 @@ CHUNKS = S // CHUNK
 EARLY = 4
 WINDOWS = 4
 SLIVER = 64
+SQUARE = 32
 
 
 def tile_list_hboth_none_kernel(tc, xT, w_words, w_scales, wgt, wgo, offs, offs2, out):
     nc = tc.nc
-    with tc.tile_pool(name="held", bufs=1) as held, tc.psum_pool(name="psum", bufs=1) as psum:
+    with (
+        tc.tile_pool(name="held", bufs=1) as held,
+        tc.tile_pool(name="placed", bufs=1) as placed,
+        tc.psum_pool(name="psum", bufs=1) as psum,
+    ):
         list_in = held.tile([P, S // 16], U16, name="list_in")
         list_out = held.tile([P, S // 16], U16, name="list_out")
         wgo_sb = held.tile([P, S], F32, name="wgo_sb")
@@ -47,19 +52,20 @@ def tile_list_hboth_none_kernel(tc, xT, w_words, w_scales, wgt, wgo, offs, offs2
         codes_half = {1: codes_late}
         y_sb = [held.tile([P, S], F32, name=f"y{b}") for b in range(BLOCKS)]
         bank = [psum.tile([P, S], F32, name=f"bank{b}") for b in range(BLOCKS)]
-        window = [held.tile([P, T], F32, name=f"window{i}", align_bytes=64) for i in range(WINDOWS)]
+        short = held.tile([P, SQUARE], F32, name="short", align_bytes=64)
+        turned = held.tile([P, SQUARE], F32, name="turned", align_bytes=64)
+        repeated = placed.tile([P, T + S], F32, name="repeated", align_bytes=64, offset=4 * T - 2 * S)
+        window = [held.tile([P, T], F32, name="window0", align_bytes=64)]
 
         nc.vector.memset(wsc[:].bitcast(I32), 0)
-        for tile in window:
-            nc.vector.memset(tile[:], 0.0)
+        nc.vector.memset(window[0][:], 0.0)
 
         rows = xT.rearrange("(a p t) n -> a t p n", p=P, t=PACK)
         words = w_words.bitcast(I32).rearrange("a p n -> p a n")
         scale_rows = w_scales.bitcast(I32).rearrange("a (q r) n -> r q a n", r=4)
         nc.sync.dma_start(plane[0][0][:], rows[0, 0])
-        nc.scalar.dma_start(wgt_sb[:, 0:CHUNK], wgt[:, 0:CHUNK])
+        nc.scalar.dma_start(short[:], wgt.rearrange("(g s) (r c) -> g s r c", s=16, c=SQUARE)[:, 0])
         nc.sync.dma_start(list_in[:], offs)
-        nc.sync.dma_start(wgt_sb[:, CHUNK:S], wgt[:, CHUNK:S])
         for a in range(PASSES):
             for t in range(PACK):
                 if a + t > 0:
@@ -71,6 +77,17 @@ def tile_list_hboth_none_kernel(tc, xT, w_words, w_scales, wgt, wgo, offs, offs2
         nc.sync.dma_start(list_out[:], offs2)
         nc.sync.dma_start(wgo_sb[:], wgo)
         nc.sync.dma_start(w_late[:].bitcast(I32), words[:, :, split : M // 2])
+
+        nc.vector.transpose(turned[:], short[:])
+        for lo in (0, HALF):
+            rs = slice(lo // SQUARE, (lo + HALF) // SQUARE)
+            src = turned[:].rearrange("p (g r) -> p r g", g=2)[:, rs].unsqueeze(3).to_broadcast([P, HALF // SQUARE, 2, 16])
+            nc.vector.tensor_copy(repeated[:, lo : lo + HALF].rearrange("p (r g s) -> p r g s", g=2, s=16), src)
+        for lo in (0, HALF):
+            nc.vector.transpose(wgt_sb[:, lo : lo + HALF], repeated[:, lo : lo + HALF])
+        for i in range(1, WINDOWS):
+            window.append(placed.tile([P, T], F32, name=f"window{i}", align_bytes=64, offset=4 * T * (i - 1)))
+            nc.gpsimd.memset(window[i][:], 0.0)
 
         def picked(a, lo, hi):
             return picks[a][:].rearrange("p (u v c) -> p u v c", u=2, v=2)[:, :, :, lo:hi]
@@ -128,7 +145,7 @@ def tile_list_hboth_none_kernel(tc, xT, w_words, w_scales, wgt, wgo, offs, offs2
 
         def store(b):
             rows_out, source = out[P * b : P * (b + 1)], window[b % WINDOWS]
-            if EARLY <= b < BLOCKS - 1:
+            if EARLY < b < BLOCKS - 1:
                 nc.sync.dma_start(rows_out, source[:])
             else:
                 second = nc.scalar if b == BLOCKS - 1 else nc.sync
@@ -136,8 +153,8 @@ def tile_list_hboth_none_kernel(tc, xT, w_words, w_scales, wgt, wgo, offs, offs2
                 second.dma_start(rows_out[:, T // 2 : T], source[:, T // 2 : T])
 
         second = [grouped_second[:, a * CHUNK * PACK : (a + 1) * CHUNK * PACK] for a in range(PASSES)]
-        gather(0, 0, 0, CHUNK)
-        gather(0, 0, CHUNK, S)
+        gather(0, 0, 0, HALF)
+        gather(0, 0, HALF, S)
         for t in range(1, PACK):
             gather(0, t, 0, S)
         interleave(grouped_first[0][:], 0, 0, CHUNK)

@@ -24,6 +24,7 @@ EARLY = 4
 WINDOWS = 4
 SLIVER = 64
 SQUARE = 32
+LEAD = 64
 
 
 def tile_list_hboth_none_kernel(tc, xT, w_words, w_scales, wgt, wgo, offs, offs2, out):
@@ -63,8 +64,9 @@ def tile_list_hboth_none_kernel(tc, xT, w_words, w_scales, wgt, wgo, offs, offs2
         rows = xT.rearrange("(a p t) n -> a t p n", p=P, t=PACK)
         words = w_words.bitcast(I32).rearrange("a p n -> p a n")
         scale_rows = w_scales.bitcast(I32).rearrange("a (q r) n -> r q a n", r=4)
-        nc.sync.dma_start(plane[0][0][:], rows[0, 0])
-        nc.scalar.dma_start(short[:], wgt.rearrange("(g s) (r c) -> g s r c", s=16, c=SQUARE)[:, 0])
+        nc.sync.dma_start(plane[0][0][:, 0:LEAD], rows[0, 0][:, 0:LEAD])
+        nc.sync.dma_start(short[:], wgt.rearrange("(g s) (r c) -> g s r c", s=16, c=SQUARE)[:, 0])
+        nc.sync.dma_start(plane[0][0][:, LEAD:T], rows[0, 0][:, LEAD:T])
         nc.sync.dma_start(list_in[:], offs)
         for a in range(PASSES):
             for t in range(PACK):
@@ -145,10 +147,10 @@ def tile_list_hboth_none_kernel(tc, xT, w_words, w_scales, wgt, wgo, offs, offs2
 
         def store(b):
             rows_out, source = out[P * b : P * (b + 1)], window[b % WINDOWS]
-            if EARLY < b < BLOCKS - 1:
+            if b in (3, 5, 6):
                 nc.sync.dma_start(rows_out, source[:])
             else:
-                second = nc.scalar if b == BLOCKS - 1 else nc.sync
+                second = nc.scalar if b >= EARLY else nc.sync
                 nc.sync.dma_start(rows_out[:, 0 : T // 2], source[:, 0 : T // 2])
                 second.dma_start(rows_out[:, T // 2 : T], source[:, T // 2 : T])
 

@@ -25,6 +25,7 @@ WINDOWS = 4
 SLIVER = 64
 SQUARE = 32
 LEAD = 64
+AHEAD = 2
 
 
 def tile_list_hboth_none_kernel(tc, xT, w_words, w_scales, wgt, wgo, offs, offs2, out):
@@ -39,7 +40,6 @@ def tile_list_hboth_none_kernel(tc, xT, w_words, w_scales, wgt, wgo, offs, offs2
         wgo_sb = held.tile([P, S], F32, name="wgo_sb")
         w_early = held.tile([P, PASSES, 2 * P * EARLY], U8, name="w_early", align_bytes=64)
         w_late = held.tile([P, PASSES, 2 * P * (BLOCKS - EARLY)], U8, name="w_late", align_bytes=64)
-        wsc = held.tile([P, PASSES, M], U8, name="wsc", align_bytes=64)
         plane = [[held.tile([P, T], F32, name=f"plane{a}_{t}", align_bytes=64) for t in range(PACK)] for a in range(PASSES)]
         picks = [held.tile([P, PACK * S], F32, name=f"picks{a}", align_bytes=64) for a in range(PASSES)]
         wgt_sb = held.tile([P, S], F32, name="wgt_sb", align_bytes=64)
@@ -53,25 +53,31 @@ def tile_list_hboth_none_kernel(tc, xT, w_words, w_scales, wgt, wgo, offs, offs2
         codes_half = {1: codes_late}
         y_sb = [held.tile([P, S], F32, name=f"y{b}") for b in range(BLOCKS)]
         bank = [psum.tile([P, S], F32, name=f"bank{b}") for b in range(BLOCKS)]
-        short = held.tile([P, SQUARE], F32, name="short", align_bytes=64)
+        short = held.tile([P, SQUARE], F32, name="short", tag="wsc", align_bytes=64)
         turned = held.tile([P, SQUARE], F32, name="turned", align_bytes=64)
-        repeated = placed.tile([P, T + S], F32, name="repeated", align_bytes=64, offset=4 * T - 2 * S)
-        window = [held.tile([P, T], F32, name="window0", align_bytes=64)]
+        repeated = placed.tile([P, S], F32, name="repeated", align_bytes=64, offset=4 * T - 2 * S)
+        window = [held.tile([P, T], F32, name=f"window{i}", align_bytes=64) for i in range(AHEAD)]
 
-        nc.vector.memset(wsc[:].bitcast(I32), 0)
-        nc.vector.memset(window[0][:], 0.0)
+        for tile in window:
+            nc.vector.memset(tile[:], 0.0)
 
         rows = xT.rearrange("(a p t) n -> a t p n", p=P, t=PACK)
         words = w_words.bitcast(I32).rearrange("a p n -> p a n")
         scale_rows = w_scales.bitcast(I32).rearrange("a (q r) n -> r q a n", r=4)
+        step = 8 * S - HALF
+        halves = wgt.rearrange("p s -> (p s)")[7 * S : 7 * S + 16 * step].rearrange("(a x) -> a x", x=step)
+        halves = halves[:, 0:HALF].rearrange("a (b c) -> a b c", c=SQUARE)
         nc.sync.dma_start(plane[0][0][:, 0:LEAD], rows[0, 0][:, 0:LEAD])
-        nc.sync.dma_start(short[:], wgt.rearrange("(g s) (r c) -> g s r c", s=16, c=SQUARE)[:, 0])
+        nc.sync.dma_start(short[:], halves)
         nc.sync.dma_start(plane[0][0][:, LEAD:T], rows[0, 0][:, LEAD:T])
         nc.sync.dma_start(list_in[:], offs)
         for a in range(PASSES):
             for t in range(PACK):
                 if a + t > 0:
                     nc.sync.dma_start(plane[a][t][:], rows[a, t])
+        nc.vector.transpose(turned[:], short[:])
+        wsc = held.tile([P, PASSES, M], U8, name="wsc", tag="wsc", align_bytes=64)
+        nc.vector.memset(wsc[:].bitcast(I32), 0)
         split = EARLY * P // 2
         nc.sync.dma_start(w_early[:].bitcast(I32), words[:, :, 0:split])
         for r in range(4):
@@ -80,15 +86,14 @@ def tile_list_hboth_none_kernel(tc, xT, w_words, w_scales, wgt, wgo, offs, offs2
         nc.sync.dma_start(wgo_sb[:], wgo)
         nc.sync.dma_start(w_late[:].bitcast(I32), words[:, :, split : M // 2])
 
-        nc.vector.transpose(turned[:], short[:])
         for lo in (0, HALF):
             rs = slice(lo // SQUARE, (lo + HALF) // SQUARE)
             src = turned[:].rearrange("p (g r) -> p r g", g=2)[:, rs].unsqueeze(3).to_broadcast([P, HALF // SQUARE, 2, 16])
             nc.vector.tensor_copy(repeated[:, lo : lo + HALF].rearrange("p (r g s) -> p r g s", g=2, s=16), src)
         for lo in (0, HALF):
             nc.vector.transpose(wgt_sb[:, lo : lo + HALF], repeated[:, lo : lo + HALF])
-        for i in range(1, WINDOWS):
-            window.append(placed.tile([P, T], F32, name=f"window{i}", align_bytes=64, offset=4 * T * (i - 1)))
+        for i in range(AHEAD, WINDOWS):
+            window.append(placed.tile([P, T], F32, name=f"window{i}", align_bytes=64, offset=4 * T * (i - AHEAD)))
             nc.gpsimd.memset(window[i][:], 0.0)
 
         def picked(a, lo, hi):

@@ -25,7 +25,7 @@ WINDOWS = 4
 SLIVER = 64
 SQUARE = 32
 LEAD = 64
-AHEAD = 2
+AHEAD = 3
 
 
 def tile_list_hboth_none_kernel(tc, xT, w_words, w_scales, wgt, wgo, offs, offs2, out):
@@ -154,6 +154,9 @@ def tile_list_hboth_none_kernel(tc, xT, w_words, w_scales, wgt, wgo, offs, offs2
             rows_out, source = out[P * b : P * (b + 1)], window[b % WINDOWS]
             if b in (3, 5, 6):
                 nc.sync.dma_start(rows_out, source[:])
+            elif b == BLOCKS - 1:
+                nc.sync.dma_start(rows_out[0:P:2], source[0:P:2])
+                nc.scalar.dma_start(rows_out[1:P:2], source[1:P:2])
             else:
                 second = nc.scalar if b >= EARLY else nc.sync
                 nc.sync.dma_start(rows_out[:, 0 : T // 2], source[:, 0 : T // 2])

@@ -37,10 +37,10 @@ def tile_list_hboth_none_kernel(tc, xT, w_words, w_scales, wgt, wgo, offs, offs2
     ):
         list_in = held.tile([P, S // 16], U16, name="list_in")
         list_out = held.tile([P, S // 16], U16, name="list_out")
-        wgo_sb = held.tile([P, S], F32, name="wgo_sb")
-        w_early = held.tile([P, PASSES, 2 * P * EARLY], U8, name="w_early", align_bytes=64)
-        w_late = held.tile([P, PASSES, 2 * P * (BLOCKS - EARLY)], U8, name="w_late", align_bytes=64)
-        plane = [[held.tile([P, T], F32, name=f"plane{a}_{t}", align_bytes=64) for t in range(PACK)] for a in range(PASSES)]
+        wgo_sb = held.tile([P, S], F32, name="wgo_sb", align_bytes=256)
+        w_early = held.tile([P, PASSES, 2 * P * EARLY], U8, name="w_early", align_bytes=256)
+        w_late = held.tile([P, PASSES, 2 * P * (BLOCKS - EARLY)], U8, name="w_late", align_bytes=256)
+        plane = [[held.tile([P, T], F32, name=f"plane{a}_{t}", align_bytes=256) for t in range(PACK)] for a in range(PASSES)]
         picks = [held.tile([P, PACK * S], F32, name=f"picks{a}", align_bytes=64) for a in range(PASSES)]
         wgt_sb = held.tile([P, S], F32, name="wgt_sb", align_bytes=64)
         grouped_first = [held.tile([P, CHUNK * PACK], BF16, name=f"grouped_first{a}", align_bytes=64) for a in range(PASSES)]
@@ -56,7 +56,7 @@ def tile_list_hboth_none_kernel(tc, xT, w_words, w_scales, wgt, wgo, offs, offs2
         short = held.tile([P, SQUARE], F32, name="short", tag="wsc", align_bytes=64)
         turned = held.tile([P, SQUARE], F32, name="turned", align_bytes=64)
         repeated = placed.tile([P, S], F32, name="repeated", align_bytes=64, offset=4 * T - 2 * S)
-        window = [held.tile([P, T], F32, name=f"window{i}", align_bytes=64) for i in range(AHEAD)]
+        window = [held.tile([P, T], F32, name=f"window{i}", align_bytes=256) for i in range(AHEAD)]
 
         for tile in window:
             nc.vector.memset(tile[:], 0.0)
@@ -93,7 +93,7 @@ def tile_list_hboth_none_kernel(tc, xT, w_words, w_scales, wgt, wgo, offs, offs2
         for lo in (0, HALF):
             nc.vector.transpose(wgt_sb[:, lo : lo + HALF], repeated[:, lo : lo + HALF])
         for i in range(AHEAD, WINDOWS):
-            window.append(placed.tile([P, T], F32, name=f"window{i}", align_bytes=64, offset=4 * T * (i - AHEAD)))
+            window.append(placed.tile([P, T], F32, name=f"window{i}", align_bytes=256, offset=4 * T * (i - AHEAD)))
             nc.gpsimd.memset(window[i][:], 0.0)
 
         def picked(a, lo, hi):

@@ -53,7 +53,7 @@ def tile_list_hboth_none_kernel(tc, xT, w_words, w_scales, wgt, wgo, offs, offs2
         codes_half = {1: codes_late}
         y_sb = [held.tile([P, S], F32, name=f"y{b}") for b in range(BLOCKS)]
         bank = [psum.tile([P, S], F32, name=f"bank{b}") for b in range(BLOCKS)]
-        short = held.tile([P, SQUARE], F32, name="short", tag="wsc", align_bytes=64)
+        short = held.tile([P, SQUARE], F32, name="short", align_bytes=64)
         turned = held.tile([P, SQUARE], F32, name="turned", align_bytes=64)
         repeated = placed.tile([P, S], F32, name="repeated", align_bytes=64, offset=4 * T - 2 * S)
         window = [held.tile([P, T], F32, name=f"window{i}", align_bytes=256) for i in range(AHEAD)]
@@ -76,8 +76,16 @@ def tile_list_hboth_none_kernel(tc, xT, w_words, w_scales, wgt, wgo, offs, offs2
                 if a + t > 0:
                     nc.sync.dma_start(plane[a][t][:], rows[a, t])
         nc.vector.transpose(turned[:], short[:])
-        wsc = held.tile([P, PASSES, M], U8, name="wsc", tag="wsc", align_bytes=64)
-        nc.vector.memset(wsc[:].bitcast(I32), 0)
+
+        pieces = ((0, CHUNK), (CHUNK, HALF), (HALF, S))
+        for lo, hi in pieces:
+            rs = slice(lo // SQUARE, hi // SQUARE)
+            src = turned[:].rearrange("p (g r) -> p r g", g=2)[:, rs].unsqueeze(3).to_broadcast([P, (hi - lo) // SQUARE, 2, 16])
+            nc.vector.tensor_copy(repeated[:, lo:hi].rearrange("p (r g s) -> p r g s", g=2, s=16), src)
+        for lo, hi in pieces:
+            nc.vector.transpose(wgt_sb[:, lo:hi], repeated[:, lo:hi])
+        wsc = placed.tile([P, PASSES, M], U8, name="wsc", align_bytes=256, offset=4 * T)
+        nc.gpsimd.memset(wsc[:].bitcast(I32), 0)
         split = EARLY * P // 2
         nc.sync.dma_start(w_early[:].bitcast(I32), words[:, :, 0:split])
         for r in range(4):
@@ -85,13 +93,6 @@ def tile_list_hboth_none_kernel(tc, xT, w_words, w_scales, wgt, wgo, offs, offs2
         nc.sync.dma_start(list_out[:], offs2)
         nc.sync.dma_start(wgo_sb[:], wgo)
         nc.sync.dma_start(w_late[:].bitcast(I32), words[:, :, split : M // 2])
-
-        for lo in (0, HALF):
-            rs = slice(lo // SQUARE, (lo + HALF) // SQUARE)
-            src = turned[:].rearrange("p (g r) -> p r g", g=2)[:, rs].unsqueeze(3).to_broadcast([P, HALF // SQUARE, 2, 16])
-            nc.vector.tensor_copy(repeated[:, lo : lo + HALF].rearrange("p (r g s) -> p r g s", g=2, s=16), src)
-        for lo in (0, HALF):
-            nc.vector.transpose(wgt_sb[:, lo : lo + HALF], repeated[:, lo : lo + HALF])
         for i in range(AHEAD, WINDOWS):
             window.append(placed.tile([P, T], F32, name=f"window{i}", align_bytes=256, offset=4 * T * (i - AHEAD)))
             nc.gpsimd.memset(window[i][:], 0.0)

@@ -24,7 +24,6 @@ EARLY = 4
 WINDOWS = 4
 SLIVER = 64
 SQUARE = 32
-LEAD = 64
 AHEAD = 3
 
 
@@ -67,9 +66,8 @@ def tile_list_hboth_none_kernel(tc, xT, w_words, w_scales, wgt, wgo, offs, offs2
         step = 8 * S - HALF
         halves = wgt.rearrange("p s -> (p s)")[7 * S : 7 * S + 16 * step].rearrange("(a x) -> a x", x=step)
         halves = halves[:, 0:HALF].rearrange("a (b c) -> a b c", c=SQUARE)
-        nc.sync.dma_start(plane[0][0][:, 0:LEAD], rows[0, 0][:, 0:LEAD])
         nc.sync.dma_start(short[:], halves)
-        nc.sync.dma_start(plane[0][0][:, LEAD:T], rows[0, 0][:, LEAD:T])
+        nc.scalar.dma_start(plane[0][0][:], rows[0, 0])
         nc.sync.dma_start(list_in[:], offs)
         for a in range(PASSES):
             for t in range(PACK):
@@ -153,7 +151,7 @@ def tile_list_hboth_none_kernel(tc, xT, w_words, w_scales, wgt, wgo, offs, offs2
 
         def store(b):
             rows_out, source = out[P * b : P * (b + 1)], window[b % WINDOWS]
-            if b in (3, 5, 6):
+            if b in (5, 6):
                 nc.sync.dma_start(rows_out, source[:])
             elif b == BLOCKS - 1:
                 nc.sync.dma_start(rows_out[0:P:2], source[0:P:2])

@@ -24,6 +24,8 @@ EARLY = 4
 WINDOWS = 4
 SLIVER = 64
 SQUARE = 32
+ROW = 4 * T
+LAP = 256
 AHEAD = 3
 
 
@@ -36,10 +38,14 @@ def tile_list_hboth_none_kernel(tc, xT, w_words, w_scales, wgt, wgo, offs, offs2
     ):
         list_in = held.tile([P, S // 16], U16, name="list_in")
         list_out = held.tile([P, S // 16], U16, name="list_out")
-        wgo_sb = held.tile([P, S], F32, name="wgo_sb", align_bytes=256)
-        w_early = held.tile([P, PASSES, 2 * P * EARLY], U8, name="w_early", align_bytes=256)
-        w_late = held.tile([P, PASSES, 2 * P * (BLOCKS - EARLY)], U8, name="w_late", align_bytes=256)
-        plane = [[held.tile([P, T], F32, name=f"plane{a}_{t}", align_bytes=256) for t in range(PACK)] for a in range(PASSES)]
+        wgo_sb = placed.tile([P, S], F32, name="wgo_sb", align_bytes=256, offset=7 * ROW)
+        w_early = placed.tile([P, PASSES, 2 * P * EARLY], U8, name="w_early", align_bytes=256, offset=6 * ROW)
+        w_late = placed.tile([P, PASSES, 2 * P * (BLOCKS - EARLY)], U8, name="w_late", align_bytes=256, offset=7 * ROW + ROW // 2)
+        places = [ROW - LAP, 4 * ROW - LAP, 6 * ROW, 7 * ROW, 0, 2 * (ROW - LAP), 3 * ROW, 5 * ROW - 2 * LAP]
+        plane = [
+            [placed.tile([P, T], F32, name=f"plane{a}_{t}", align_bytes=256, offset=places[PACK * a + t]) for t in range(PACK)]
+            for a in range(PASSES)
+        ]
         picks = [held.tile([P, PACK * S], F32, name=f"picks{a}", align_bytes=64) for a in range(PASSES)]
         wgt_sb = held.tile([P, S], F32, name="wgt_sb", align_bytes=64)
         grouped_first = [held.tile([P, CHUNK * PACK], BF16, name=f"grouped_first{a}", align_bytes=64) for a in range(PASSES)]
@@ -54,7 +60,7 @@ def tile_list_hboth_none_kernel(tc, xT, w_words, w_scales, wgt, wgo, offs, offs2
         bank = [psum.tile([P, S], F32, name=f"bank{b}") for b in range(BLOCKS)]
         short = held.tile([P, SQUARE], F32, name="short", align_bytes=64)
         turned = held.tile([P, SQUARE], F32, name="turned", align_bytes=64)
-        repeated = placed.tile([P, S], F32, name="repeated", align_bytes=64, offset=4 * T - 2 * S)
+        repeated = placed.tile([P, S], F32, name="repeated", align_bytes=64, offset=8 * ROW)
         window = [held.tile([P, T], F32, name=f"window{i}", align_bytes=256) for i in range(AHEAD)]
 
         for tile in window:
@@ -67,12 +73,10 @@ def tile_list_hboth_none_kernel(tc, xT, w_words, w_scales, wgt, wgo, offs, offs2
         halves = wgt.rearrange("p s -> (p s)")[7 * S : 7 * S + 16 * step].rearrange("(a x) -> a x", x=step)
         halves = halves[:, 0:HALF].rearrange("a (b c) -> a b c", c=SQUARE)
         nc.sync.dma_start(short[:], halves)
-        nc.scalar.dma_start(plane[0][0][:], rows[0, 0])
         nc.sync.dma_start(list_in[:], offs)
-        for a in range(PASSES):
-            for t in range(PACK):
-                if a + t > 0:
-                    nc.sync.dma_start(plane[a][t][:], rows[a, t])
+        nc.sync.dma_start(list_out[:], offs2)
+        for t in range(PACK):
+            nc.scalar.dma_start(plane[0][t][:], rows[0, t])
         nc.vector.transpose(turned[:], short[:])
 
         pieces = ((0, CHUNK), (CHUNK, HALF), (HALF, S))
@@ -82,17 +86,8 @@ def tile_list_hboth_none_kernel(tc, xT, w_words, w_scales, wgt, wgo, offs, offs2
             nc.vector.tensor_copy(repeated[:, lo:hi].rearrange("p (r g s) -> p r g s", g=2, s=16), src)
         for lo, hi in pieces:
             nc.vector.transpose(wgt_sb[:, lo:hi], repeated[:, lo:hi])
-        wsc = placed.tile([P, PASSES, M], U8, name="wsc", align_bytes=256, offset=4 * T)
-        nc.gpsimd.memset(wsc[:].bitcast(I32), 0)
-        split = EARLY * P // 2
-        nc.sync.dma_start(w_early[:].bitcast(I32), words[:, :, 0:split])
-        for r in range(4):
-            nc.sync.dma_start(wsc[r:P:32].bitcast(I32), scale_rows[r])
-        nc.sync.dma_start(list_out[:], offs2)
-        nc.sync.dma_start(wgo_sb[:], wgo)
-        nc.sync.dma_start(w_late[:].bitcast(I32), words[:, :, split : M // 2])
         for i in range(AHEAD, WINDOWS):
-            window.append(placed.tile([P, T], F32, name=f"window{i}", align_bytes=256, offset=4 * T * (i - AHEAD)))
+            window.append(placed.tile([P, T], F32, name=f"window{i}", align_bytes=256, offset=ROW * (8 + i - AHEAD)))
             nc.gpsimd.memset(window[i][:], 0.0)
 
         def picked(a, lo, hi):
@@ -164,8 +159,21 @@ def tile_list_hboth_none_kernel(tc, xT, w_words, w_scales, wgt, wgo, offs, offs2
         second = [grouped_second[:, a * CHUNK * PACK : (a + 1) * CHUNK * PACK] for a in range(PASSES)]
         gather(0, 0, 0, HALF)
         gather(0, 0, HALF, S)
-        for t in range(1, PACK):
-            gather(0, t, 0, S)
+        for t in (0, 1):
+            nc.sync.dma_start(plane[1][t][:], rows[1, t])
+        gather(0, 1, 0, S)
+        for t in (2, 3):
+            nc.sync.dma_start(plane[1][t][:], rows[1, t])
+        gather(0, 2, 0, S)
+        wsc = placed.tile([P, PASSES, M], U8, name="wsc", align_bytes=256, offset=6 * ROW + ROW // 2)
+        nc.gpsimd.memset(wsc[:].bitcast(I32), 0)
+        split = EARLY * P // 2
+        nc.sync.dma_start(w_early[:].bitcast(I32), words[:, :, 0:split])
+        for r in range(4):
+            nc.sync.dma_start(wsc[r:P:32].bitcast(I32), scale_rows[r])
+        gather(0, 3, 0, S)
+        nc.sync.dma_start(wgo_sb[:], wgo)
+        nc.sync.dma_start(w_late[:].bitcast(I32), words[:, :, split : M // 2])
         interleave(grouped_first[0][:], 0, 0, CHUNK)
         interleave(second[0], 0, CHUNK, HALF)
         interleave(grouped_half[:], 0, HALF, S)

@@ -26,7 +26,7 @@ SLIVER = 64
 SQUARE = 32
 ROW = 4 * T
 LAP = 256
-AHEAD = 3
+AHEAD = 2
 
 
 def tile_list_hboth_none_kernel(tc, xT, w_words, w_scales, wgt, wgo, offs, offs2, out):
@@ -60,7 +60,7 @@ def tile_list_hboth_none_kernel(tc, xT, w_words, w_scales, wgt, wgo, offs, offs2
         bank = [psum.tile([P, S], F32, name=f"bank{b}") for b in range(BLOCKS)]
         short = held.tile([P, SQUARE], F32, name="short", align_bytes=64)
         turned = held.tile([P, SQUARE], F32, name="turned", align_bytes=64)
-        repeated = placed.tile([P, S], F32, name="repeated", align_bytes=64, offset=8 * ROW)
+        repeated = placed.tile([P, S], F32, name="repeated", align_bytes=64, offset=9 * ROW - 2 * S)
         window = [held.tile([P, T], F32, name=f"window{i}", align_bytes=256) for i in range(AHEAD)]
 
         for tile in window:

import concourse.mybir as mybir

K, M, T, S = 1024, 1024, 1024, 512
FLOPS = 2 * K * M * S

F32 = mybir.dt.float32
BF16 = mybir.dt.bfloat16
I32 = mybir.dt.int32
U32 = mybir.dt.uint32
U16 = mybir.dt.uint16
U8 = mybir.dt.uint8
FP8X4 = mybir.dt.float8_e4m3fn_x4
FP4X4 = mybir.dt.float4_e2m1fn_x4
MULT = mybir.AluOpType.mult

P = 128
PACK = 4
PASSES = K // (P * PACK)
BLOCKS = M // P
HALF = S // 2
CHUNK = 128
CHUNKS = S // CHUNK
EARLY = 4
WINDOWS = 4
SLIVER = 64
SQUARE = 32
ROW = 4 * T
LAP = 256
AHEAD = 2


def tile_list_hboth_none_kernel(tc, xT, w_words, w_scales, wgt, wgo, offs, offs2, out):
    nc = tc.nc
    with (
        tc.tile_pool(name="held", bufs=1) as held,
        tc.tile_pool(name="placed", bufs=1) as placed,
        tc.psum_pool(name="psum", bufs=1) as psum,
    ):
        list_in = held.tile([P, S // 16], U16, name="list_in")
        list_out = held.tile([P, S // 16], U16, name="list_out")
        wgo_sb = placed.tile([P, S], F32, name="wgo_sb", align_bytes=256, offset=7 * ROW)
        w_early = placed.tile([P, PASSES, 2 * P * EARLY], U8, name="w_early", align_bytes=256, offset=6 * ROW)
        w_late = placed.tile([P, PASSES, 2 * P * (BLOCKS - EARLY)], U8, name="w_late", align_bytes=256, offset=7 * ROW + ROW // 2)
        places = [ROW - LAP, 4 * ROW - LAP, 6 * ROW, 7 * ROW, 0, 2 * (ROW - LAP), 3 * ROW, 5 * ROW - 2 * LAP]
        plane = [
            [placed.tile([P, T], F32, name=f"plane{a}_{t}", align_bytes=256, offset=places[PACK * a + t]) for t in range(PACK)]
            for a in range(PASSES)
        ]
        picks = [held.tile([P, PACK * S], F32, name=f"picks{a}", align_bytes=64) for a in range(PASSES)]
        wgt_sb = held.tile([P, S], F32, name="wgt_sb", align_bytes=64)
        grouped_first = [held.tile([P, CHUNK * PACK], BF16, name=f"grouped_first{a}", align_bytes=64) for a in range(PASSES)]
        grouped_second = held.tile([P, PASSES * CHUNK * PACK], BF16, name="grouped_second", align_bytes=64)
        grouped_half = held.tile([P, HALF * PACK], BF16, name="grouped_half", align_bytes=64)
        grouped_late = held.tile([P, SLIVER * PACK], BF16, name="grouped_late", align_bytes=64)
        codes_front = held.tile([P, PASSES * HALF], U32, name="codes_front", align_bytes=64)
        codes_late = held.tile([P, HALF], U32, name="codes_late", align_bytes=64)
        xsc = held.tile([P, PASSES * S], U8, name="xsc", align_bytes=64)
        codes_half = {1: codes_late}
        y_sb = [held.tile([P, S], F32, name=f"y{b}") for b in range(BLOCKS)]
        bank = [psum.tile([P, S], F32, name=f"bank{b}") for b in range(BLOCKS)]
        short = held.tile([P, SQUARE], F32, name="short", align_bytes=64)
        turned = held.tile([P, SQUARE], F32, name="turned", align_bytes=64)
        repeated = placed.tile([P, S], F32, name="repeated", align_bytes=64, offset=9 * ROW - 2 * S)
        window = [held.tile([P, T], F32, name=f"window{i}", align_bytes=256) for i in range(AHEAD)]

        for tile in window:
            nc.vector.memset(tile[:], 0.0)

        rows = xT.rearrange("(a p t) n -> a t p n", p=P, t=PACK)
        words = w_words.bitcast(I32).rearrange("a p n -> p a n")
        scale_rows = w_scales.bitcast(I32).rearrange("a (q r) n -> r q a n", r=4)
        step = 8 * S - HALF
        halves = wgt.rearrange("p s -> (p s)")[7 * S : 7 * S + 16 * step].rearrange("(a x) -> a x", x=step)
        halves = halves[:, 0:HALF].rearrange("a (b c) -> a b c", c=SQUARE)
        nc.sync.dma_start(short[:], halves)
        nc.sync.dma_start(list_in[:], offs)
        nc.sync.dma_start(list_out[:], offs2)
        for t in range(PACK):
            nc.scalar.dma_start(plane[0][t][:], rows[0, t])
        nc.vector.transpose(turned[:], short[:])

        pieces = ((0, CHUNK), (CHUNK, HALF), (HALF, S))
        for lo, hi in pieces:
            rs = slice(lo // SQUARE, hi // SQUARE)
            src = turned[:].rearrange("p (g r) -> p r g", g=2)[:, rs].unsqueeze(3).to_broadcast([P, (hi - lo) // SQUARE, 2, 16])
            nc.vector.tensor_copy(repeated[:, lo:hi].rearrange("p (r g s) -> p r g s", g=2, s=16), src)
        for lo, hi in pieces:
            nc.vector.transpose(wgt_sb[:, lo:hi], repeated[:, lo:hi])
        for i in range(AHEAD, WINDOWS):
            window.append(placed.tile([P, T], F32, name=f"window{i}", align_bytes=256, offset=ROW * (8 + i - AHEAD)))
            nc.gpsimd.memset(window[i][:], 0.0)

        def picked(a, lo, hi):
            return picks[a][:].rearrange("p (u v c) -> p u v c", u=2, v=2)[:, :, :, lo:hi]

        def left(a, t, lo, hi):
            return picks[a][:, t * S + lo : t * S + hi]

        last_pair = picks[1][:, 2 * S : 3 * S].rearrange("p (v c) -> p v c", v=2)[:, :, 0:CHUNK]

        def gather(a, t, lo, hi, dst=None):
            nc.vector.tensor_tensor(
                picked(a, lo, hi)[:, t // 2, t % 2, :] if dst is None else dst,
                plane[a][t][:].indirect(list_in[:, lo // 16 : hi // 16]),
                wgt_sb[:, lo:hi],
                MULT,
            )

        def interleave(grouped, a, lo, hi, pairs=slice(0, 2)):
            dst = grouped.rearrange("p (c i u v) -> p c u v i", i=4, u=2, v=2)
            src = picked(a, lo, hi).rearrange("p u v (c i) -> p c u v i", i=4)
            nc.scalar.copy(dst[:, :, pairs], src[:, :, pairs])

        def operand(a, lo, width):
            if lo < HALF:
                at = PASSES * lo + a * CHUNK
                return codes_front[:, at : at + width].bitcast(FP8X4), xsc[:, at : at + width]
            at = (PASSES + a - 1) * HALF + lo
            return codes_half[a][:, lo - HALF : lo - HALF + width].bitcast(FP8X4), xsc[:, at : at + width]

        def quantize(a, lo, width, grouped):
            codes, scales = operand(a, lo, width)
            nc.vector.quantize_mx(out=codes, scales=scales, in_=grouped)

        def multiply(b, c):
            w_sb, first = (w_early, b) if b < EARLY else (w_late, b - EARLY)
            order = range(PASSES) if b < 2 else range(PASSES - 1, -1, -1)
            for a in order:
                codes, scales = operand(a, c, CHUNK)
                nc.tensor.matmul_mx(
                    out=bank[b][:, c : c + CHUNK],
                    lhsT=w_sb[:, a, 2 * P * first : 2 * P * (first + 1)].bitcast(FP4X4),
                    lhsT_scale=wsc[:, a, P * b : P * (b + 1)],
                    rhs=codes,
                    rhs_scale=scales,
                    start=(a == order[0]),
                    stop=(a == order[-1]),
                )

        def place(b, lo, hi, y):
            chunks = range(lo, hi, CHUNK)
            for c in chunks if b < 2 else reversed(chunks):
                multiply(b, c)
            nc.scalar.copy(y, bank[b][:, lo:hi])
            nc.vector.tensor_tensor(window[b % WINDOWS][:].indirect(list_out[:, lo // 16 : hi // 16]), y, wgo_sb[:, lo:hi], MULT)

        def store(b):
            rows_out, source = out[P * b : P * (b + 1)], window[b % WINDOWS]
            if b in (5, 6):
                nc.sync.dma_start(rows_out, source[:])
            elif b == BLOCKS - 1:
                nc.sync.dma_start(rows_out[0:P:2], source[0:P:2])
                nc.scalar.dma_start(rows_out[1:P:2], source[1:P:2])
            else:
                second = nc.scalar if b >= EARLY else nc.sync
                nc.sync.dma_start(rows_out[:, 0 : T // 2], source[:, 0 : T // 2])
                second.dma_start(rows_out[:, T // 2 : T], source[:, T // 2 : T])

        second = [grouped_second[:, a * CHUNK * PACK : (a + 1) * CHUNK * PACK] for a in range(PASSES)]
        gather(0, 0, 0, HALF)
        gather(0, 0, HALF, S)
        for t in (0, 1):
            nc.sync.dma_start(plane[1][t][:], rows[1, t])
        gather(0, 1, 0, S)
        for t in (2, 3):
            nc.sync.dma_start(plane[1][t][:], rows[1, t])
        gather(0, 2, 0, S)
        wsc = placed.tile([P, PASSES, M], U8, name="wsc", align_bytes=256, offset=6 * ROW + ROW // 2)
        nc.gpsimd.memset(wsc[:].bitcast(I32), 0)
        split = EARLY * P // 2
        nc.sync.dma_start(w_early[:].bitcast(I32), words[:, :, 0:split])
        for r in range(4):
            nc.sync.dma_start(wsc[r:P:32].bitcast(I32), scale_rows[r])
        gather(0, 3, 0, S)
        nc.sync.dma_start(wgo_sb[:], wgo)
        nc.sync.dma_start(w_late[:].bitcast(I32), words[:, :, split : M // 2])
        interleave(grouped_first[0][:], 0, 0, CHUNK)
        interleave(second[0], 0, CHUNK, HALF)
        interleave(grouped_half[:], 0, HALF, S)
        gather(1, 0, 0, S)
        quantize(0, 0, CHUNK, grouped_first[0][:])
        gather(1, 1, 0, S)
        interleave(grouped_first[1][:], 1, 0, CHUNK, slice(0, 1))
        interleave(second[1], 1, CHUNK, HALF, slice(0, 1))
        gather(1, 2, 0, HALF)
        gather(1, 3, 0, CHUNK, last_pair[:, 1, :])
        gather(1, 3, CHUNK, S)
        nc.scalar.copy(
            grouped_first[1][:].rearrange("p (c i u v) -> p c u v i", i=4, u=2, v=2)[:, :, 1],
            last_pair.rearrange("p v (c i) -> p c v i", i=4),
        )
        interleave(second[1], 1, CHUNK, HALF, slice(1, 2))
        quantize(1, 0, CHUNK, grouped_first[1][:])
        gather(1, 2, HALF, S)
        codes_half[0] = held.tile([P, HALF], U32, name="codes_half", tag="grouped_first1", align_bytes=64)
        quantize(0, HALF, HALF, grouped_half[:])
        quantize(0, CHUNK, PASSES * CHUNK, grouped_second[:])

        slivers = range(HALF, S, SLIVER)
        steps = [(b, lo) for lo in (0, CHUNK) for b in range(EARLY)]
        staged = [y_sb[b][:, lo : lo + CHUNK] for b, lo in steps]
        staged[0] = grouped_late[:].bitcast(F32)
        grouped = [grouped_late[:]]
        for i, lo in enumerate(slivers):
            staged[i + 3] = left(1, i, lo - SLIVER, lo + SLIVER)
            if i > 0:
                grouped.append(left(1, (i + 1) % PACK, lo - 2 * SLIVER, lo).bitcast(BF16))
        staged[-1] = left(1, 1, S - CHUNK, S)
        for i, (b, lo) in enumerate(steps):
            place(b, lo, lo + CHUNK, staged[i])
            if 2 <= i < 2 + len(slivers):
                at = slivers[i - 2]
                interleave(grouped[i - 2], 1, at, at + SLIVER)
                quantize(1, at, SLIVER, grouped[i - 2])
        for b in range(EARLY):
            place(b, HALF, S, y_sb[b][:, HALF:S])
            store(b)
        for b in range(EARLY, BLOCKS):
            place(b, 0, S, y_sb[b][:])
            store(b)
